import numpy as np
import ml_dtypes


def mxq(x, axis, fmt="e4m3"):
    dtype, down = {"e4m3": (ml_dtypes.float8_e4m3fn, 7), "e5m2": (ml_dtypes.float8_e5m2, 14)}[fmt]
    v = np.moveaxis(np.asarray(x, np.float32).astype(ml_dtypes.bfloat16).astype(np.float64), axis, -1)
    blocks = v.reshape(v.shape[:-1] + (-1, 32))
    amax = np.abs(blocks).max(-1, keepdims=True)
    byte = np.maximum(np.where(amax > 0, np.frexp(amax)[1] - 1 + 127, 0) - down, 1)
    scale = np.exp2(byte - 127.0)
    codes = (blocks / scale).astype(np.float32).astype(dtype).astype(np.float64)
    return np.moveaxis((codes * scale).reshape(v.shape), -1, axis)


WIDE = False


def mx_kscale(k):
    if not WIDE:
        return np.ones(k)
    levels = np.array([10, -10, 5, -5, 0])
    if k % 512:
        return np.exp2(np.random.permutation(np.resize(levels, k // 32))).repeat(32)
    a = np.empty((k // 512, 16))
    for p in range(k // 512):
        a[p, :8] = np.random.permutation(np.resize(levels, 8))
        for g in range(8):
            far = levels[np.abs(levels - a[p, g]) >= 10]
            a[p, g + 8] = far[np.random.randint(len(far))]
    return np.exp2(a.ravel()).repeat(32)


def f64(x):
    return np.asarray(x).astype(np.float64)


def striped(idx):
    return np.tile(idx.reshape(-1, 16).T, (8, 1)).astype(np.uint16)


def unstriped(offs):
    return offs[:16].T.reshape(-1).astype(np.int64)


E2M1 = np.array([0.0, 0.5, 1.0, 1.5, 2.0, 3.0, 4.0, 6.0, -0.0, -0.5, -1.0, -1.5, -2.0, -3.0, -4.0, -6.0])


def pack_weight(w, fmt):
    k, n = w.shape
    w = f64(np.asarray(w, np.float32).astype(ml_dtypes.bfloat16)).reshape(k // 32, 32, n)
    amax = np.abs(w).max(1)
    if fmt == "e4m3":
        byte = np.frexp(amax)[1] - 1 + 127 - 7
    else:
        mant, ex = np.frexp(amax / 6.0)
        byte = np.where(mant > 0.5, ex, ex - 1) + 127
    byte = np.clip(np.where(amax > 0, byte, 1), 1, 254)
    scaled = (w * np.exp2(127.0 - byte)[:, None, :]).reshape(k, n).astype(np.float32)
    by_word = np.ascontiguousarray(scaled.reshape(k // 512, 128, 4, n).transpose(0, 1, 3, 2))
    if fmt == "e4m3":
        words = by_word.astype(ml_dtypes.float8_e4m3fn).view(np.uint8)
    else:
        c = by_word.astype(ml_dtypes.float4_e2m1fn).view(np.uint8) & 0xF
        words = (c[..., 0::2] | (c[..., 1::2] << 4)).reshape(k // 512, 128, 2 * n)
    return np.ascontiguousarray(words), np.ascontiguousarray(byte.astype(np.uint8).reshape(k // 512, 16, n))


def unpack_weight(words, scales, fmt):
    g, _, n = scales.shape
    words = np.ascontiguousarray(words).reshape(g, 128, n, -1)
    if fmt == "e4m3":
        vals = words.view(ml_dtypes.float8_e4m3fn).astype(np.float64)
    else:
        nib = np.empty((g, 128, n, 4), np.uint8)
        nib[..., 0::2] = words & 0xF
        nib[..., 1::2] = words >> 4
        vals = E2M1[nib]
    vals = vals * np.repeat(np.exp2(scales.astype(np.float64) - 127.0), 8, axis=1)[..., None]
    return vals.transpose(0, 1, 3, 2).reshape(g * 512, n)


def gelu(v):
    return 0.5 * v * (1.0 + np.tanh(np.sqrt(2.0 / np.pi) * (v + 0.044715 * v**3)))


def often(T, S):
    return np.random.permutation(T)[(T * np.random.uniform(0, 1, S) ** 4).astype(np.int64)]


def bf(x):
    return np.asarray(x, np.float32).astype(ml_dtypes.bfloat16)


def planes(Y):
    n, m = Y.shape
    b = f64(bf(Y)).reshape(n // 32, 32, m)
    amax = np.abs(b).max(1)
    byte = np.clip(np.where(amax > 0, np.frexp(amax)[1] - 1 + 127 - 7, 1), 1, 254)
    codes = (b * np.exp2(127.0 - byte)[:, None, :]).reshape(n, m).astype(np.float32).astype(ml_dtypes.float8_e4m3fn).view(np.uint8)
    words = codes.reshape(n // 512, 128, 4, m).transpose(0, 1, 3, 2)
    return np.ascontiguousarray(words), np.ascontiguousarray(byte.astype(np.uint8).reshape(n // 512, 16, m))


K, K2, H, N, T, S, T2, P = 1024, 512, 1024, 1024, 4096, 1024, 2048, 512

def setup_inputs():
    n = np.random.standard_normal
    s, s2, u = mx_kscale(K)[:, None], mx_kscale(K2)[:, None], mx_kscale(H)[:, None]
    tab_words, tab_scales = pack_weight(n((K, T)) * s, "e4m3")
    tab2_words, tab2_scales = pack_weight(n((K2, T2)) * s2, "e4m3")
    w1_words, w1_scales = pack_weight(n((K, H)) / np.sqrt(K) / s, "e2m1")
    w3_words, w3_scales = pack_weight(n((H, H)) / np.sqrt(H) / u, "e4m3")
    return {
        "tab_words": tab_words, "tab_scales": tab_scales,
        "offs": striped(np.random.permutation(T)[:S]),
        "pos1": striped(often(S, P)),
        "tab2_words": tab2_words, "tab2_scales": tab2_scales,
        "offs2": striped(np.random.permutation(T2)[:P]),
        "w1_words": w1_words, "w1_scales": w1_scales,
        "w2": (n((K2, H)) / np.sqrt(K2) / s2).astype(np.float32),
        "w3_words": w3_words, "w3_scales": w3_scales,
        "gain": (np.random.uniform(0.5, 2.0, H) * u[:, 0]).astype(np.float32),
        "w4": (0.5 * n((H, N)) / np.sqrt(H) / u * np.exp(0.8 * n(N))).astype(np.float32),
    }

def reference(tab_words, tab_scales, offs, pos1, tab2_words, tab2_scales, offs2,
              w1_words, w1_scales, w2, w3_words, w3_scales, gain, w4):
    v = unpack_weight(tab_words, tab_scales, "e4m3")[:, unstriped(offs)]
    v2 = unpack_weight(tab2_words, tab2_scales, "e4m3")[:, unstriped(offs2)]
    h = unpack_weight(w1_words, w1_scales, "e2m1").T @ v
    a = h[:, unstriped(pos1)]
    w2q = mxq(f64(w2), 0, "e4m3")
    b = w2q.T @ v2
    gv = f64(gain)[:, None]
    e1 = np.tanh(a + b)
    f1 = mxq(gv * e1, 0, "e4m3")
    e2 = np.tanh(unpack_weight(w3_words, w3_scales, "e4m3").T @ f1 + w2q.T @ v2)
    z = gv * (e1 + e2)
    y = mxq(f64(w4), 0, "e4m3").T @ mxq(z, 0, "e4m3")
    words, scales = planes(y)
    return y, words, scales

@@ -1,0 +1,309 @@
+from contextlib import ExitStack
+
+import concourse.mybir as mybir
+
+K, K2, H, N, T, S, T2, NL = 1024, 512, 1024, 1024, 4096, 1024, 2048, 512
+FLOPS = 5368709120
+
+F32 = mybir.dt.float32
+BF16 = mybir.dt.bfloat16
+I32 = mybir.dt.int32
+U32 = mybir.dt.uint32
+U16 = mybir.dt.uint16
+U8 = mybir.dt.uint8
+FP8X4 = mybir.dt.float8_e4m3fn_x4
+FP4X4 = mybir.dt.float4_e2m1fn_x4
+ACT = mybir.ActivationFunctionType
+ALU = mybir.AluOpType
+
+P = 128
+PACK = 4
+GROUP = P * PACK
+BANK = 512
+HALF = 256
+
+
+def tile_list_root_lateral_slopes_kernel(
+    tc, tab_words, tab_scales, offs, pos1, tab2_words, tab2_scales, offs2,
+    w1_words, w1_scales, w2, w3_words, w3_scales, gain, w4, out_0, out_1, out_2,
+):
+    nc = tc.nc
+    with ExitStack() as ctx:
+        lists = ctx.enter_context(tc.tile_pool(name="lists", bufs=1))
+        keep = ctx.enter_context(tc.tile_pool(name="keep", bufs=1))
+        ring = ctx.enter_context(tc.tile_pool(name="ring", bufs=1))
+        psum = ctx.enter_context(tc.psum_pool(name="psum", bufs=8))
+
+        def kept(name, shape, dtype):
+            return keep.tile(shape, dtype, name=name, align_bytes=64)
+
+        def bank(shape):
+            return psum.tile(shape, F32, name="bank", tag="bank")
+
+        def page(shape):
+            return ring.tile(shape, F32, name="page", tag="page", bufs=10, align_bytes=64)
+
+        def woven(width):
+            return ring.tile([P, width], BF16, name="woven", tag="woven", bufs=4, align_bytes=64)
+
+        idx = lists.tile([P, S // 16], U16, name="idx")
+        p1 = lists.tile([P, NL // 16], U16, name="p1")
+        idx2 = lists.tile([P, NL // 16], U16, name="idx2")
+
+        w1s_raw = kept("w1s_raw", [P, 2, H], U8)
+        tabs = kept("tabs", [P, 2, T], U8)
+        tab2s = kept("tab2s", [P, T2], U8)
+        w3s_raw = kept("w3s_raw", [P, H], U8)
+        nc.vector.memset(tabs[:].rearrange("p a c -> p (a c)").bitcast(I32), 0)
+        nc.gpsimd.memset(w1s_raw[:].rearrange("p a c -> p (a c)").bitcast(I32), 0)
+        warm = kept("warm", [P, 1], F32)
+        nc.vector.memset(warm[:], 0.0)
+        nc.scalar.activation(warm[:], warm[:], ACT.Tanh)
+        nc.gpsimd.memset(tab2s[:].bitcast(I32), 0)
+        nc.gpsimd.memset(w3s_raw[:].bitcast(I32), 0)
+
+        gains = kept("gains", [P, 2, PACK], F32)
+        w1w_raw = kept("w1w_raw", [P, 2, 2 * H], U8)
+        tabw = [kept(f"tabw{a}", [P, T], U32) for a in range(2)]
+        tab2w = kept("tab2w", [P, T2], U32)
+        w3w_raw = [kept(f"w3w_raw{a}", [P, H], I32) for a in range(2)]
+
+        def load_table(a, lo, hi):
+            nc.sync.dma_start(
+                tabw[a][:, lo:hi].bitcast(I32), tab_words[a].rearrange("p n t -> p (n t)").bitcast(I32)[:, lo:hi]
+            )
+
+        def load_scale_rows(queue, tile, rows):
+            for q in range(4):
+                queue.dma_start(tile[32 * q : 32 * q + 4].bitcast(I32), rows[4 * q : 4 * q + 4].bitcast(I32))
+
+        def load_weight(rows, g):
+            raw = ring.tile([P, PACK, GROUP], F32, name="wraw", tag="wraw", bufs=4)
+            nc.sync.dma_start(raw[:], rows[:, g * GROUP : (g + 1) * GROUP].rearrange("(p j) c -> p j c", j=PACK))
+            return raw
+
+        nc.sync.dma_start(idx[:], offs)
+        nc.sync.dma_start(w1w_raw[:].bitcast(I32), w1_words.rearrange("a p c -> p a c").bitcast(I32))
+        load_scale_rows(nc.sync, tabs[:], tab_scales.rearrange("a q c -> q a c"))
+        load_table(0, 0, 2048)
+        load_scale_rows(nc.sync, w1s_raw[:], w1_scales.rearrange("a q c -> q a c"))
+        load_table(0, 2048, 4096)
+        nc.sync.dma_start(idx2[:], offs2)
+        nc.sync.dma_start(p1[:], pos1)
+        nc.sync.dma_start(gains[:], gain.rearrange("(g p t) -> p g t", g=2, t=PACK))
+        load_table(1, 0, 1536)
+        load_scale_rows(nc.sync, tab2s[:], tab2_scales[0])
+        load_table(1, 1536, 3072)
+        for q in range(4):
+            nc.sync.dma_start(w3s_raw[32 * q : 32 * q + 8, :].bitcast(I32), w3_scales[:, 4 * q : 4 * q + 4, :].bitcast(I32))
+        load_table(1, 3072, 4096)
+        nc.sync.dma_start(tab2w[:].bitcast(I32), tab2_words[0].rearrange("p n t -> p (n t)").bitcast(I32))
+        w2_raw = [load_weight(w2, g) for g in range(2)]
+        for a in range(2):
+            nc.sync.dma_start(w3w_raw[a][:], w3_words[a].rearrange("p n t -> p (n t)").bitcast(I32))
+        w4_raw = [[load_weight(w4[GROUP * a : GROUP * (a + 1), :], g) for a in range(2)] for g in range(2)]
+
+        w1w = [kept(f"w1w{a}", [P, 2 * H], U8) for a in range(2)]
+        w1s = kept("w1s", [P, 2, H], U8)
+        for a in range(2):
+            nc.vector.tensor_copy(
+                w1w[a][:].bitcast(U16).rearrange("p (g t m) -> p g t m", g=2, t=PACK),
+                w1w_raw[:, a, :].bitcast(U16).rearrange("p (g m t) -> p g t m", g=2, t=PACK),
+            )
+        nc.vector.tensor_copy(
+            w1s[:].rearrange("p a (g t m) -> p (a g) t m", g=2, t=PACK),
+            w1s_raw[:].rearrange("p a (g m t) -> p (a g) t m", g=2, t=PACK),
+        )
+
+        v = [[kept(f"v{a}{u}", [P, BANK], U32) for u in range(2)] for a in range(2)]
+        v_scales = [kept(f"vs{a}", [P, S], U8) for a in range(2)]
+        for a in range(2):
+            nc.vector.tensor_copy(v_scales[a][:], tabs[:, a, :].indirect(idx[:]))
+            for u in range(2):
+                nc.vector.tensor_copy(v[a][u][:], tabw[a][:].indirect(idx[:, 32 * u : 32 * (u + 1)]))
+
+        h = [page([P, S]) for s in range(8)]
+
+        def h_pass(acc, s, u, a):
+            nc.tensor.matmul_mx(
+                acc[:],
+                lhsT=w1w[a][:, 2 * P * s : 2 * P * (s + 1)].bitcast(FP4X4),
+                lhsT_scale=w1s[:, a, P * s : P * (s + 1)],
+                rhs=v[a][u][:].bitcast(FP8X4),
+                rhs_scale=v_scales[a][:, BANK * u : BANK * (u + 1)],
+                start=(a == 0), stop=(a == 1),
+            )
+
+        early = {}
+        for u in range(2):
+            for s in range(4):
+                early[(s, u)] = bank([P, BANK])
+                h_pass(early[(s, u)], s, u, 0)
+        for u in range(2):
+            for s in range(4):
+                h_pass(early[(s, u)], s, u, 1)
+        for s in range(4):
+            for u in range(2):
+                nc.scalar.copy(h[s][:, BANK * u : BANK * (u + 1)], early[(s, u)][:])
+        for s in range(4, 8):
+            for u in range(2):
+                acc = bank([P, BANK])
+                h_pass(acc, s, u, 0)
+                h_pass(acc, s, u, 1)
+                nc.scalar.copy(h[s][:, BANK * u : BANK * (u + 1)], acc[:])
+
+        v2 = kept("v2", [P, NL], U32)
+        v2s = kept("v2s", [P, NL], U8)
+        nc.vector.tensor_copy(v2s[:], tab2s[:].indirect(idx2[:]))
+        nc.vector.tensor_copy(v2[:], tab2w[:].indirect(idx2[:]))
+
+        def quantise_weight(raw, name, copies):
+            wi = woven(PACK * GROUP)
+            dst = wi[:].rearrange("p (t m j) -> p m j t", t=PACK, j=PACK)
+            src = raw[:].rearrange("p j (m t) -> p m j t", t=PACK)
+            step = P // len(copies)
+            for i, copy in enumerate(copies):
+                copy(dst[:, step * i : step * (i + 1)], src[:, step * i : step * (i + 1)])
+            codes = kept(name + "c", [P, GROUP], U32)
+            scales = kept(name + "s", [P, GROUP], U8)
+            nc.vector.quantize_mx(codes[:].bitcast(FP8X4), scales[:], wi[:])
+            return codes, scales
+
+        on_vector, on_scalar = nc.vector.tensor_copy, nc.scalar.copy
+        w2q = [quantise_weight(w2_raw[g], f"w2q{g}", [on_vector]) for g in range(2)]
+
+        def lateral_pass(acc, g, t, cols, alone):
+            codes, scales = w2q[g]
+            nc.tensor.matmul_mx(
+                acc,
+                lhsT=codes[:, P * t : P * (t + 1)].bitcast(FP8X4),
+                lhsT_scale=scales[:, P * t : P * (t + 1)],
+                rhs=v2[:, cols].bitcast(FP8X4),
+                rhs_scale=v2s[:, cols],
+                start=alone, stop=alone,
+            )
+
+        def quantise_rows(rows, codes, scales, copy):
+            width = rows.shape[2]
+            wi = woven(PACK * width)
+            copy(
+                wi[:].rearrange("p (c i t) -> p c t i", i=4, t=PACK),
+                rows.rearrange("p t (c i) -> p c t i", i=4),
+            )
+            nc.vector.quantize_mx(codes.bitcast(FP8X4), scales, wi[:])
+
+        e1 = [kept(f"e1{g}", [P, PACK, NL], F32) for g in range(2)]
+        f1_codes = [kept(f"f1c{g}", [P, NL], U32) for g in range(2)]
+        f1_scales = [kept(f"f1s{g}", [P, NL], U8) for g in range(2)]
+
+        def first_slope(g):
+            rows = e1[g]
+            for t in range(PACK):
+                row = rows[:, t, :]
+                nc.vector.tensor_copy(row, h[PACK * g + t][:].indirect(p1[:]))
+                acc = bank([P, NL])
+                lateral_pass(acc[:], g, t, slice(0, NL), True)
+                nc.vector.tensor_tensor(row, acc[:], row, ALU.add)
+                nc.scalar.activation(row, row, ACT.Tanh)
+                if (g, t) in [(0,0),(0,1),(0,2),(0,3)]:
+                    nc.scalar.activation(row, row, ACT.Copy, scale=gains[:, g, t : t + 1])
+                else:
+                    nc.vector.tensor_scalar(row, row, gains[:, g, t : t + 1], None, ALU.mult)
+            quantise_rows(rows[:], f1_codes[g][:], f1_scales[g][:], [on_scalar,on_vector][g])
+
+        w3w = [kept(f"w3w{a}", [P, H], I32) for a in range(2)]
+        w3s = kept("w3s", [P, H], U8)
+
+        def deal_w3():
+            for a in range(2):
+                nc.vector.tensor_copy(
+                    w3w[a][:].rearrange("p (g t c i) -> p g c t i", g=2, t=PACK, i=4),
+                    w3w_raw[a][:].rearrange("p (g c i t) -> p g c t i", g=2, t=PACK, i=4),
+                )
+            nc.vector.tensor_copy(
+                w3s[:].rearrange("p (g t m) -> p g t m", g=2, t=PACK),
+                w3s_raw[:].rearrange("p (g m t) -> p g t m", g=2, t=PACK),
+            )
+
+        def second_slope(lo, width):
+            cols = slice(lo, lo + width)
+            per_bank = BANK // width
+            z = []
+            for g in range(2):
+                rows = page([P, PACK, width])
+                for t0 in range(0, PACK, per_bank):
+                    acc = bank([P, per_bank, width])
+                    for a in range(2):
+                        for i in range(per_bank):
+                            t = t0 + i
+                            w_cols = slice(GROUP * g + P * t, GROUP * g + P * (t + 1))
+                            nc.tensor.matmul_mx(
+                                acc[:, i, :],
+                                lhsT=w3w[a][:, w_cols].bitcast(FP8X4),
+                                lhsT_scale=w3s[4 * a : P, w_cols],
+                                rhs=f1_codes[a][:, cols].bitcast(FP8X4),
+                                rhs_scale=f1_scales[a][:, cols],
+                                start=(a == 0 and i == 0), stop=(a == 1 and i == per_bank - 1),
+                            )
+                            if a == 0:
+                                lateral_pass(acc[:, i, :], g, t, cols, False)
+                    nc.scalar.activation(rows[:, t0 : t0 + per_bank, :], acc[:], ACT.Tanh)
+                for t in range(PACK):
+                    nc.vector.scalar_tensor_tensor(
+                        rows[:, t, :], rows[:, t, :], gains[:, g, t : t + 1], e1[g][:, t, cols], ALU.mult, ALU.add
+                    )
+                codes = kept(f"zc{lo}{g}", [P, width], U32)
+                scales = kept(f"zs{lo}{g}", [P, width], U8)
+                quantise_rows(rows[:], codes[:], scales[:], on_vector)
+                z.append((codes, scales))
+            return z
+
+        y_scales = kept("y_scales", [P, 2, NL], U8)
+
+        def result(lo, width, z, w4q, copy, empty):
+            cols = slice(lo, lo + width)
+            per_bank = BANK // width
+            for g in range(2):
+                rows = page([P, PACK, width])
+                for t0 in range(0, PACK, per_bank):
+                    acc = bank([P, per_bank, width])
+                    for a in range(2):
+                        for i in range(per_bank):
+                            t = t0 + i
+                            codes, scales = w4q[a][g]
+                            nc.tensor.matmul_mx(
+                                acc[:, i, :],
+                                lhsT=codes[:, P * t : P * (t + 1)].bitcast(FP8X4),
+                                lhsT_scale=scales[:, P * t : P * (t + 1)],
+                                rhs=z[a][0][:].bitcast(FP8X4),
+                                rhs_scale=z[a][1][:],
+                                start=(a == 0 and i == 0), stop=(a == 1 and i == per_bank - 1),
+                            )
+                    empty[g](rows[:, t0 : t0 + per_bank, :], acc[:])
+                nc.sync.dma_start(
+                    out_0[GROUP * g : GROUP * (g + 1), cols].rearrange("(p t) m -> p t m", t=PACK), rows[:]
+                )
+                y_codes = kept(f"yc{lo}{g}", [P, width], U32)
+                quantise_rows(rows[:], y_codes[:], y_scales[:, g, cols], copy[g])
+                nc.sync.dma_start(
+                    out_1[g, :, cols, :].rearrange("p m t -> p (m t)").bitcast(I32), y_codes[:].bitcast(I32)
+                )
+
+        w4q = [[None, None], [None, None]]
+        w4c = [[on_scalar]*2]*3+[[on_vector]]
+        first_slope(0)
+        first_slope(1)
+        deal_w3()
+        w4q[0][0] = quantise_weight(w4_raw[0][0], "w4q0", w4c[0])
+        w4q[1][0] = quantise_weight(w4_raw[0][1], "w4q1", w4c[1])
+        w4q[0][1] = quantise_weight(w4_raw[1][0], "w4q2", w4c[2])
+        w4q[1][1] = quantise_weight(w4_raw[1][1], "w4q3", w4c[3])
+        chunks = [(0,256),(256,256)]
+        z = [second_slope(lo, width) for lo, width in chunks]
+        for k, (lo, width) in enumerate(chunks):
+            result(lo, width, z[k], w4q, [[on_scalar,on_scalar],[on_vector,on_vector]][k], [[on_scalar,on_scalar],[on_scalar,on_scalar]][k])
+        for q in range(4):
+            nc.sync.dma_start(
+                out_2[:, 4 * q : 4 * q + 4, :].rearrange("g r m -> r g m").bitcast(I32),
+                y_scales[32 * q : 32 * q + 4, :, :].bitcast(I32),
+            )

@@ -51,14 +51,13 @@ def tile_list_root_lateral_slopes_kernel(
         idx2 = lists.tile([P, NL // 16], U16, name="idx2")
 
         w1s_raw = kept("w1s_raw", [P, 2, H], U8)
-        tabs = kept("tabs", [P, 2, T], U8)
+        tabs = kept("tabs", [P, T], U8)
+        v_scales = [kept(f"vs{a}", [P, S], U8) for a in range(2)]
         tab2s = kept("tab2s", [P, T2], U8)
         w3s_raw = kept("w3s_raw", [P, H], U8)
-        nc.vector.memset(tabs[:].rearrange("p a c -> p (a c)").bitcast(I32), 0)
+        nc.vector.memset(tabs[:].bitcast(I32), 0)
         nc.gpsimd.memset(w1s_raw[:].rearrange("p a c -> p (a c)").bitcast(I32), 0)
-        warm = kept("warm", [P, 1], F32)
-        nc.vector.memset(warm[:], 0.0)
-        nc.scalar.activation(warm[:], warm[:], ACT.Tanh)
+        nc.gpsimd.memset(v_scales[1][:].bitcast(I32), 0)
         nc.gpsimd.memset(tab2s[:].bitcast(I32), 0)
         nc.gpsimd.memset(w3s_raw[:].bitcast(I32), 0)
 
@@ -78,30 +77,36 @@ def tile_list_root_lateral_slopes_kernel(
                 queue.dma_start(tile[32 * q : 32 * q + 4].bitcast(I32), rows[4 * q : 4 * q + 4].bitcast(I32))
 
         def load_weight(rows, g):
-            raw = ring.tile([P, PACK, GROUP], F32, name="wraw", tag="wraw", bufs=4)
+            raw = ring.tile([P, PACK, GROUP], F32, name="wraw", tag="wraw", bufs=5)
             nc.sync.dma_start(raw[:], rows[:, g * GROUP : (g + 1) * GROUP].rearrange("(p j) c -> p j c", j=PACK))
             return raw
 
         nc.sync.dma_start(idx[:], offs)
         nc.sync.dma_start(w1w_raw[:].bitcast(I32), w1_words.rearrange("a p c -> p a c").bitcast(I32))
-        load_scale_rows(nc.sync, tabs[:], tab_scales.rearrange("a q c -> q a c"))
+        for q in range(4):
+            nc.sync.dma_start(tabs[32 * q : 32 * q + 8, :].bitcast(I32), tab_scales[:, 4 * q : 4 * q + 4, :].bitcast(I32))
         load_table(0, 0, 2048)
         load_scale_rows(nc.sync, w1s_raw[:], w1_scales.rearrange("a q c -> q a c"))
         load_table(0, 2048, 4096)
         nc.sync.dma_start(idx2[:], offs2)
         nc.sync.dma_start(p1[:], pos1)
         nc.sync.dma_start(gains[:], gain.rearrange("(g p t) -> p g t", g=2, t=PACK))
-        load_table(1, 0, 1536)
+        load_table(1, 0, 2048)
         load_scale_rows(nc.sync, tab2s[:], tab2_scales[0])
-        load_table(1, 1536, 3072)
+        load_table(1, 2048, 4096)
+        nc.vector.tensor_copy(v_scales[0][:], tabs[:].indirect(idx[:]))
         for q in range(4):
-            nc.sync.dma_start(w3s_raw[32 * q : 32 * q + 8, :].bitcast(I32), w3_scales[:, 4 * q : 4 * q + 4, :].bitcast(I32))
-        load_table(1, 3072, 4096)
+            nc.sync.dma_start(
+                v_scales[1][32 * q : 32 * q + 4, :].bitcast(I32), v_scales[0][32 * q + 4 : 32 * q + 8, :].bitcast(I32)
+            )
         nc.sync.dma_start(tab2w[:].bitcast(I32), tab2_words[0].rearrange("p n t -> p (n t)").bitcast(I32))
         w2_raw = [load_weight(w2, g) for g in range(2)]
+        w4_raw = [[load_weight(w4[GROUP * a : GROUP * (a + 1), :], 0) for a in range(2)]]
+        for q in range(4):
+            nc.sync.dma_start(w3s_raw[32 * q : 32 * q + 8, :].bitcast(I32), w3_scales[:, 4 * q : 4 * q + 4, :].bitcast(I32))
         for a in range(2):
             nc.sync.dma_start(w3w_raw[a][:], w3_words[a].rearrange("p n t -> p (n t)").bitcast(I32))
-        w4_raw = [[load_weight(w4[GROUP * a : GROUP * (a + 1), :], g) for a in range(2)] for g in range(2)]
+        w4_raw.append([load_weight(w4[GROUP * a : GROUP * (a + 1), :], 1) for a in range(2)])
 
         w1w = [kept(f"w1w{a}", [P, 2 * H], U8) for a in range(2)]
         w1s = kept("w1s", [P, 2, H], U8)
@@ -116,9 +121,7 @@ def tile_list_root_lateral_slopes_kernel(
         )
 
         v = [[kept(f"v{a}{u}", [P, BANK], U32) for u in range(2)] for a in range(2)]
-        v_scales = [kept(f"vs{a}", [P, S], U8) for a in range(2)]
         for a in range(2):
-            nc.vector.tensor_copy(v_scales[a][:], tabs[:, a, :].indirect(idx[:]))
             for u in range(2):
                 nc.vector.tensor_copy(v[a][u][:], tabw[a][:].indirect(idx[:, 32 * u : 32 * (u + 1)]))
 
@@ -209,7 +212,9 @@ def tile_list_root_lateral_slopes_kernel(
                     nc.scalar.activation(row, row, ACT.Copy, scale=gains[:, g, t : t + 1])
                 else:
                     nc.vector.tensor_scalar(row, row, gains[:, g, t : t + 1], None, ALU.mult)
-            quantise_rows(rows[:], f1_codes[g][:], f1_scales[g][:], [on_scalar,on_vector][g])
+            for lo, width in [[(0,512)],[(0,256),(256,256)]][g]:
+                cols = slice(lo, lo + width)
+                quantise_rows(rows[:, :, cols], f1_codes[g][:, cols], f1_scales[g][:, cols], [on_scalar,on_vector][g])
 
         w3w = [kept(f"w3w{a}", [P, H], I32) for a in range(2)]
         w3s = kept("w3s", [P, H], U8)
@@ -225,7 +230,7 @@ def tile_list_root_lateral_slopes_kernel(
                 w3s_raw[:].rearrange("p (g m t) -> p g t m", g=2, t=PACK),
             )
 
-        def second_slope(lo, width):
+        def second_slope(lo, width, copy):
             cols = slice(lo, lo + width)
             per_bank = BANK // width
             z = []
@@ -254,7 +259,7 @@ def tile_list_root_lateral_slopes_kernel(
                     )
                 codes = kept(f"zc{lo}{g}", [P, width], U32)
                 scales = kept(f"zs{lo}{g}", [P, width], U8)
-                quantise_rows(rows[:], codes[:], scales[:], on_vector)
+                quantise_rows(rows[:], codes[:], scales[:], copy[g])
                 z.append((codes, scales))
             return z
 
@@ -290,20 +295,20 @@ def tile_list_root_lateral_slopes_kernel(
                 )
 
         w4q = [[None, None], [None, None]]
-        w4c = [[on_scalar]*2]*3+[[on_vector]]
+        w4c = [[on_scalar]*2]*4
+        w4q[0][0] = quantise_weight(w4_raw[0][0], "w4q0", w4c[0])
+        w4q[1][0] = quantise_weight(w4_raw[0][1], "w4q1", w4c[1])
         first_slope(0)
         first_slope(1)
         deal_w3()
-        w4q[0][0] = quantise_weight(w4_raw[0][0], "w4q0", w4c[0])
-        w4q[1][0] = quantise_weight(w4_raw[0][1], "w4q1", w4c[1])
         w4q[0][1] = quantise_weight(w4_raw[1][0], "w4q2", w4c[2])
         w4q[1][1] = quantise_weight(w4_raw[1][1], "w4q3", w4c[3])
         chunks = [(0,256),(256,256)]
-        z = [second_slope(lo, width) for lo, width in chunks]
+        z = [second_slope(lo, width, [[on_scalar,on_vector],[on_vector,on_vector]][k]) for k, (lo, width) in enumerate(chunks)]
         for k, (lo, width) in enumerate(chunks):
-            result(lo, width, z[k], w4q, [[on_scalar,on_scalar],[on_vector,on_vector]][k], [[on_scalar,on_scalar],[on_scalar,on_scalar]][k])
+            result(lo, width, z[k], w4q, [[on_scalar,on_vector],[on_scalar,on_vector]][k], [[on_scalar,on_scalar],[on_scalar,on_vector]][k])
         for q in range(4):
-            nc.sync.dma_start(
+            (nc.sync, nc.scalar)[q % 2].dma_start(
                 out_2[:, 4 * q : 4 * q + 4, :].rearrange("g r m -> r g m").bitcast(I32),
                 y_scales[32 * q : 32 * q + 4, :, :].bitcast(I32),
             )

@@ -2,7 +2,9 @@ from contextlib import ExitStack
 
 import concourse.mybir as mybir
 
-K, K2, H, N, T, S, T2, NL = 1024, 512, 1024, 1024, 4096, 1024, 2048, 512
+H = 1024
+T, S = 4096, 1024
+T2, NL = 2048, 512
 FLOPS = 5368709120
 
 F32 = mybir.dt.float32
@@ -19,8 +21,15 @@ ALU = mybir.AluOpType
 P = 128
 PACK = 4
 GROUP = P * PACK
+GROUPS = H // GROUP
+QUADS = 4
 BANK = 512
-HALF = 256
+BANKS = 8
+PER_COLUMN = 16
+HALF = NL // 2
+LINE = 4
+RAW_BUFS = 4
+WOVEN_BUFS = 5
 
 
 def tile_list_root_lateral_slopes_kernel(
@@ -28,11 +37,12 @@ def tile_list_root_lateral_slopes_kernel(
     w1_words, w1_scales, w2, w3_words, w3_scales, gain, w4, out_0, out_1, out_2,
 ):
     nc = tc.nc
+    on_vector, on_scalar = nc.vector.tensor_copy, nc.scalar.copy
     with ExitStack() as ctx:
         lists = ctx.enter_context(tc.tile_pool(name="lists", bufs=1))
         keep = ctx.enter_context(tc.tile_pool(name="keep", bufs=1))
         ring = ctx.enter_context(tc.tile_pool(name="ring", bufs=1))
-        psum = ctx.enter_context(tc.psum_pool(name="psum", bufs=8))
+        psum = ctx.enter_context(tc.psum_pool(name="psum", bufs=BANKS))
 
         def kept(name, shape, dtype):
             return keep.tile(shape, dtype, name=name, align_bytes=64)
@@ -41,139 +51,122 @@ def tile_list_root_lateral_slopes_kernel(
             return psum.tile(shape, F32, name="bank", tag="bank")
 
         def page(shape):
-            return ring.tile(shape, F32, name="page", tag="page", bufs=10, align_bytes=64)
+            return ring.tile(shape, F32, name="page", tag="page", bufs=GROUPS * PACK, align_bytes=64)
 
         def woven(width):
-            return ring.tile([P, width], BF16, name="woven", tag="woven", bufs=4, align_bytes=64)
+            return ring.tile([P, width], BF16, name="woven", tag="woven", bufs=WOVEN_BUFS, align_bytes=64)
 
-        idx = lists.tile([P, S // 16], U16, name="idx")
-        p1 = lists.tile([P, NL // 16], U16, name="p1")
-        idx2 = lists.tile([P, NL // 16], U16, name="idx2")
+        idx = lists.tile([P, S // PER_COLUMN], U16, name="idx")
+        p1 = lists.tile([P, NL // PER_COLUMN], U16, name="p1")
+        idx2 = lists.tile([P, NL // PER_COLUMN], U16, name="idx2")
 
-        w1s_raw = kept("w1s_raw", [P, 2, H], U8)
-        tabs = kept("tabs", [P, T], U8)
-        v_scales = [kept(f"vs{a}", [P, S], U8) for a in range(2)]
-        tab2s = kept("tab2s", [P, T2], U8)
-        w3s_raw = kept("w3s_raw", [P, H], U8)
-        nc.vector.memset(tabs[:].bitcast(I32), 0)
-        nc.gpsimd.memset(w1s_raw[:].rearrange("p a c -> p (a c)").bitcast(I32), 0)
-        nc.gpsimd.memset(v_scales[1][:].bitcast(I32), 0)
-        nc.gpsimd.memset(tab2s[:].bitcast(I32), 0)
-        nc.gpsimd.memset(w3s_raw[:].bitcast(I32), 0)
+        w1_scale_raw = kept("w1_scale_raw", [P, GROUPS, H], U8)
+        tab_scale_rows = kept("tab_scale_rows", [P, T], U8)
+        v_scales = [kept(f"v_scales{a}", [P, S], U8) for a in range(GROUPS)]
+        tab2_scale_plane = kept("tab2_scale_plane", [P, T2], U8)
+        w3_scale_raw = kept("w3_scale_raw", [P, H], U8)
+        nc.vector.memset(tab2_scale_plane[:].bitcast(I32), 0)
+        nc.vector.memset(tab_scale_rows[:].bitcast(I32), 0)
+        nc.gpsimd.memset(w1_scale_raw[:].rearrange("p a c -> p (a c)").bitcast(I32), 0)
+        for a in range(GROUPS):
+            nc.gpsimd.memset(v_scales[a][:].bitcast(I32), 0)
+        nc.gpsimd.memset(w3_scale_raw[:].bitcast(I32), 0)
 
-        gains = kept("gains", [P, 2, PACK], F32)
-        w1w_raw = kept("w1w_raw", [P, 2, 2 * H], U8)
-        tabw = [kept(f"tabw{a}", [P, T], U32) for a in range(2)]
-        tab2w = kept("tab2w", [P, T2], U32)
-        w3w_raw = [kept(f"w3w_raw{a}", [P, H], I32) for a in range(2)]
+        gains = kept("gains", [P, GROUPS, PACK], F32)
+        w1_raw = kept("w1_raw", [P, GROUPS, 2 * H], U8)
+        tab_sb = [kept(f"tab_sb{a}", [P, T], U32) for a in range(GROUPS)]
+        tab2_sb = kept("tab2_sb", [P, T2], U32)
+        w3_raw = [kept(f"w3_raw{a}", [P, H], I32) for a in range(GROUPS)]
 
-        def load_table(a, lo, hi):
-            nc.sync.dma_start(
-                tabw[a][:, lo:hi].bitcast(I32), tab_words[a].rearrange("p n t -> p (n t)").bitcast(I32)[:, lo:hi]
-            )
+        def as_words(packed):
+            return packed.rearrange("p n t -> p (n t)").bitcast(I32)
 
-        def load_scale_rows(queue, tile, rows):
-            for q in range(4):
-                queue.dma_start(tile[32 * q : 32 * q + 4].bitcast(I32), rows[4 * q : 4 * q + 4].bitcast(I32))
+        def load_table_half(a, half):
+            cols = slice(half * T // 2, (half + 1) * T // 2)
+            nc.sync.dma_start(tab_sb[a][:, cols].bitcast(I32), as_words(tab_words[a])[:, cols])
+
+        def place_scale_rows(plane, rows):
+            for q in range(QUADS):
+                nc.sync.dma_start(plane[32 * q : 32 * q + 4].bitcast(I32), rows[4 * q : 4 * q + 4].bitcast(I32))
 
         def load_weight(rows, g):
-            raw = ring.tile([P, PACK, GROUP], F32, name="wraw", tag="wraw", bufs=5)
+            raw = ring.tile([P, PACK, GROUP], F32, name="raw", tag="raw", bufs=RAW_BUFS)
             nc.sync.dma_start(raw[:], rows[:, g * GROUP : (g + 1) * GROUP].rearrange("(p j) c -> p j c", j=PACK))
             return raw
 
-        nc.sync.dma_start(idx[:], offs)
-        nc.sync.dma_start(w1w_raw[:].bitcast(I32), w1_words.rearrange("a p c -> p a c").bitcast(I32))
-        for q in range(4):
-            nc.sync.dma_start(tabs[32 * q : 32 * q + 8, :].bitcast(I32), tab_scales[:, 4 * q : 4 * q + 4, :].bitcast(I32))
-        load_table(0, 0, 2048)
-        load_scale_rows(nc.sync, w1s_raw[:], w1_scales.rearrange("a q c -> q a c"))
-        load_table(0, 2048, 4096)
         nc.sync.dma_start(idx2[:], offs2)
+        nc.sync.dma_start(tab2_sb[:].bitcast(I32), as_words(tab2_words[0]))
+        nc.sync.dma_start(idx[:], offs)
+        place_scale_rows(tab2_scale_plane[:], tab2_scales[0])
+        nc.sync.dma_start(
+            tab_scale_rows[0 : 16 * GROUPS, :].bitcast(I32), tab_scales.rearrange("a q c -> (a q) c").bitcast(I32)
+        )
+        w2_raw = [load_weight(w2, 0)]
+        place_scale_rows(w1_scale_raw[:], w1_scales.rearrange("a q c -> q a c"))
+        w2_raw.append(load_weight(w2, 1))
+        nc.sync.dma_start(w1_raw[:].bitcast(I32), w1_words.rearrange("a p c -> p a c").bitcast(I32))
         nc.sync.dma_start(p1[:], pos1)
-        nc.sync.dma_start(gains[:], gain.rearrange("(g p t) -> p g t", g=2, t=PACK))
-        load_table(1, 0, 2048)
-        load_scale_rows(nc.sync, tab2s[:], tab2_scales[0])
-        load_table(1, 2048, 4096)
-        nc.vector.tensor_copy(v_scales[0][:], tabs[:].indirect(idx[:]))
-        for q in range(4):
+        nc.sync.dma_start(gains[:], gain.rearrange("(g p t) -> p g t", g=GROUPS, t=PACK))
+        load_table_half(0, 0)
+        v_scale_rows = kept("v_scale_rows", [P, S], U8)
+        nc.vector.tensor_copy(v_scale_rows[:], tab_scale_rows[:].indirect(idx[:]))
+        place_scale_rows(v_scales[0][:], v_scale_rows[0:16, :])
+        load_table_half(0, 1)
+        place_scale_rows(v_scales[1][:], v_scale_rows[16:32, :])
+        load_table_half(1, 0)
+        for q in range(QUADS):
             nc.sync.dma_start(
-                v_scales[1][32 * q : 32 * q + 4, :].bitcast(I32), v_scales[0][32 * q + 4 : 32 * q + 8, :].bitcast(I32)
+                w3_scale_raw[32 * q : 32 * q + 8, :].bitcast(I32), w3_scales[:, 4 * q : 4 * q + 4, :].bitcast(I32)
             )
-        nc.sync.dma_start(tab2w[:].bitcast(I32), tab2_words[0].rearrange("p n t -> p (n t)").bitcast(I32))
-        w2_raw = [load_weight(w2, g) for g in range(2)]
-        w4_raw = [[load_weight(w4[GROUP * a : GROUP * (a + 1), :], 0) for a in range(2)]]
-        for q in range(4):
-            nc.sync.dma_start(w3s_raw[32 * q : 32 * q + 8, :].bitcast(I32), w3_scales[:, 4 * q : 4 * q + 4, :].bitcast(I32))
-        for a in range(2):
-            nc.sync.dma_start(w3w_raw[a][:], w3_words[a].rearrange("p n t -> p (n t)").bitcast(I32))
-        w4_raw.append([load_weight(w4[GROUP * a : GROUP * (a + 1), :], 1) for a in range(2)])
+        load_table_half(1, 1)
+        for a in range(GROUPS):
+            nc.sync.dma_start(w3_raw[a][:], as_words(w3_words[a]))
+        w4_raw = {(a, g): load_weight(w4[GROUP * a : GROUP * (a + 1), :], g) for g in range(GROUPS) for a in range(GROUPS)}
 
-        w1w = [kept(f"w1w{a}", [P, 2 * H], U8) for a in range(2)]
-        w1s = kept("w1s", [P, 2, H], U8)
-        for a in range(2):
+        w1_codes = [kept(f"w1_codes{a}", [P, 2 * H], U8) for a in range(GROUPS)]
+        w1_plane = kept("w1_plane", [P, GROUPS, H], U8)
+        for a in range(GROUPS):
             nc.vector.tensor_copy(
-                w1w[a][:].bitcast(U16).rearrange("p (g t m) -> p g t m", g=2, t=PACK),
-                w1w_raw[:, a, :].bitcast(U16).rearrange("p (g m t) -> p g t m", g=2, t=PACK),
+                w1_codes[a][:].bitcast(U16).rearrange("p (g t m) -> p g t m", g=GROUPS, t=PACK),
+                w1_raw[:, a, :].bitcast(U16).rearrange("p (g m t) -> p g t m", g=GROUPS, t=PACK),
             )
         nc.vector.tensor_copy(
-            w1s[:].rearrange("p a (g t m) -> p (a g) t m", g=2, t=PACK),
-            w1s_raw[:].rearrange("p a (g m t) -> p (a g) t m", g=2, t=PACK),
+            w1_plane[:].rearrange("p a (g t m) -> p (a g) t m", g=GROUPS, t=PACK),
+            w1_scale_raw[:].rearrange("p a (g m t) -> p (a g) t m", g=GROUPS, t=PACK),
         )
 
-        v = [[kept(f"v{a}{u}", [P, BANK], U32) for u in range(2)] for a in range(2)]
-        for a in range(2):
-            for u in range(2):
-                nc.vector.tensor_copy(v[a][u][:], tabw[a][:].indirect(idx[:, 32 * u : 32 * (u + 1)]))
+        v_codes = {}
+        for a in range(GROUPS):
+            for u in range(S // BANK):
+                v_codes[a, u] = kept(f"v_codes{a}{u}", [P, BANK], U32)
+                entries = idx[:, u * BANK // PER_COLUMN : (u + 1) * BANK // PER_COLUMN]
+                nc.vector.tensor_copy(v_codes[a, u][:], tab_sb[a][:].indirect(entries))
+        v2_codes = kept("v2_codes", [P, NL], U32)
+        v2_scales = kept("v2_scales", [P, NL], U8)
+        nc.vector.tensor_copy(v2_scales[:], tab2_scale_plane[:].indirect(idx2[:]))
+        nc.vector.tensor_copy(v2_codes[:], tab2_sb[:].indirect(idx2[:]))
 
-        h = [page([P, S]) for s in range(8)]
-
-        def h_pass(acc, s, u, a):
-            nc.tensor.matmul_mx(
-                acc[:],
-                lhsT=w1w[a][:, 2 * P * s : 2 * P * (s + 1)].bitcast(FP4X4),
-                lhsT_scale=w1s[:, a, P * s : P * (s + 1)],
-                rhs=v[a][u][:].bitcast(FP8X4),
-                rhs_scale=v_scales[a][:, BANK * u : BANK * (u + 1)],
-                start=(a == 0), stop=(a == 1),
-            )
-
-        early = {}
-        for u in range(2):
-            for s in range(4):
-                early[(s, u)] = bank([P, BANK])
-                h_pass(early[(s, u)], s, u, 0)
-        for u in range(2):
-            for s in range(4):
-                h_pass(early[(s, u)], s, u, 1)
-        for s in range(4):
-            for u in range(2):
-                nc.scalar.copy(h[s][:, BANK * u : BANK * (u + 1)], early[(s, u)][:])
-        for s in range(4, 8):
-            for u in range(2):
-                acc = bank([P, BANK])
-                h_pass(acc, s, u, 0)
-                h_pass(acc, s, u, 1)
-                nc.scalar.copy(h[s][:, BANK * u : BANK * (u + 1)], acc[:])
-
-        v2 = kept("v2", [P, NL], U32)
-        v2s = kept("v2s", [P, NL], U8)
-        nc.vector.tensor_copy(v2s[:], tab2s[:].indirect(idx2[:]))
-        nc.vector.tensor_copy(v2[:], tab2w[:].indirect(idx2[:]))
-
-        def quantise_weight(raw, name, copies):
-            wi = woven(PACK * GROUP)
-            dst = wi[:].rearrange("p (t m j) -> p m j t", t=PACK, j=PACK)
+        def quantise_weight(raw, name, copy, pieces):
+            staged = woven(PACK * GROUP)
+            dst = staged[:].rearrange("p (t m j) -> p m j t", t=PACK, j=PACK)
             src = raw[:].rearrange("p j (m t) -> p m j t", t=PACK)
-            step = P // len(copies)
-            for i, copy in enumerate(copies):
-                copy(dst[:, step * i : step * (i + 1)], src[:, step * i : step * (i + 1)])
-            codes = kept(name + "c", [P, GROUP], U32)
-            scales = kept(name + "s", [P, GROUP], U8)
-            nc.vector.quantize_mx(codes[:].bitcast(FP8X4), scales[:], wi[:])
+            step = P // pieces
+            for m0 in range(0, P, step):
+                copy(dst[:, m0 : m0 + step], src[:, m0 : m0 + step])
+            codes = kept(name + "_codes", [P, GROUP], U32)
+            scales = kept(name + "_scales", [P, GROUP], U8)
+            nc.vector.quantize_mx(codes[:].bitcast(FP8X4), scales[:], staged[:])
             return codes, scales
 
-        on_vector, on_scalar = nc.vector.tensor_copy, nc.scalar.copy
-        w2q = [quantise_weight(w2_raw[g], f"w2q{g}", [on_vector]) for g in range(2)]
+        def quantise_rows(rows, codes, scales, copy):
+            staged = woven(PACK * rows.shape[2])
+            copy(
+                staged[:].rearrange("p (c i t) -> p c t i", i=LINE, t=PACK),
+                rows.rearrange("p t (c i) -> p c t i", i=LINE),
+            )
+            nc.vector.quantize_mx(codes.bitcast(FP8X4), scales, staged[:])
+
+        w2q = [quantise_weight(w2_raw[g], f"w2q{g}", on_scalar, 1) for g in range(GROUPS)]
 
         def lateral_pass(acc, g, t, cols, alone):
             codes, scales = w2q[g]
@@ -181,133 +174,140 @@ def tile_list_root_lateral_slopes_kernel(
                 acc,
                 lhsT=codes[:, P * t : P * (t + 1)].bitcast(FP8X4),
                 lhsT_scale=scales[:, P * t : P * (t + 1)],
-                rhs=v2[:, cols].bitcast(FP8X4),
-                rhs_scale=v2s[:, cols],
+                rhs=v2_codes[:, cols].bitcast(FP8X4),
+                rhs_scale=v2_scales[:, cols],
                 start=alone, stop=alone,
             )
 
-        def quantise_rows(rows, codes, scales, copy):
-            width = rows.shape[2]
-            wi = woven(PACK * width)
-            copy(
-                wi[:].rearrange("p (c i t) -> p c t i", i=4, t=PACK),
-                rows.rearrange("p t (c i) -> p c t i", i=4),
-            )
-            nc.vector.quantize_mx(codes.bitcast(FP8X4), scales, wi[:])
-
-        e1 = [kept(f"e1{g}", [P, PACK, NL], F32) for g in range(2)]
-        f1_codes = [kept(f"f1c{g}", [P, NL], U32) for g in range(2)]
-        f1_scales = [kept(f"f1s{g}", [P, NL], U8) for g in range(2)]
-
-        def first_slope(g):
-            rows = e1[g]
+        b = {}
+        for g in range(GROUPS):
             for t in range(PACK):
-                row = rows[:, t, :]
-                nc.vector.tensor_copy(row, h[PACK * g + t][:].indirect(p1[:]))
                 acc = bank([P, NL])
                 lateral_pass(acc[:], g, t, slice(0, NL), True)
-                nc.vector.tensor_tensor(row, acc[:], row, ALU.add)
-                nc.scalar.activation(row, row, ACT.Tanh)
-                if (g, t) in [(0,0),(0,1),(0,2),(0,3)]:
-                    nc.scalar.activation(row, row, ACT.Copy, scale=gains[:, g, t : t + 1])
-                else:
-                    nc.vector.tensor_scalar(row, row, gains[:, g, t : t + 1], None, ALU.mult)
-            for lo, width in [[(0,512)],[(0,256),(256,256)]][g]:
-                cols = slice(lo, lo + width)
-                quantise_rows(rows[:, :, cols], f1_codes[g][:, cols], f1_scales[g][:, cols], [on_scalar,on_vector][g])
+                b[g, t] = kept(f"b{g}{t}", [P, NL], F32)
+                nc.scalar.copy(b[g, t][:], acc[:])
 
-        w3w = [kept(f"w3w{a}", [P, H], I32) for a in range(2)]
-        w3s = kept("w3s", [P, H], U8)
+        h = [page([P, S]) for s in range(GROUPS * PACK)]
 
-        def deal_w3():
-            for a in range(2):
-                nc.vector.tensor_copy(
-                    w3w[a][:].rearrange("p (g t c i) -> p g c t i", g=2, t=PACK, i=4),
-                    w3w_raw[a][:].rearrange("p (g c i t) -> p g c t i", g=2, t=PACK, i=4),
-                )
-            nc.vector.tensor_copy(
-                w3s[:].rearrange("p (g t m) -> p g t m", g=2, t=PACK),
-                w3s_raw[:].rearrange("p (g m t) -> p g t m", g=2, t=PACK),
+        def mother_pass(acc, s, u, a):
+            nc.tensor.matmul_mx(
+                acc[:],
+                lhsT=w1_codes[a][:, 2 * P * s : 2 * P * (s + 1)].bitcast(FP4X4),
+                lhsT_scale=w1_plane[:, a, P * s : P * (s + 1)],
+                rhs=v_codes[a, u][:].bitcast(FP8X4),
+                rhs_scale=v_scales[a][:, BANK * u : BANK * (u + 1)],
+                start=(a == 0), stop=(a == GROUPS - 1),
             )
 
-        def second_slope(lo, width, copy):
-            cols = slice(lo, lo + width)
-            per_bank = BANK // width
-            z = []
-            for g in range(2):
-                rows = page([P, PACK, width])
+        first = {(s, u): bank([P, BANK]) for u in range(S // BANK) for s in range(PACK)}
+        for a in range(GROUPS):
+            for (s, u), acc in first.items():
+                mother_pass(acc, s, u, a)
+        for s in range(PACK):
+            for u in range(S // BANK):
+                nc.scalar.copy(h[s][:, BANK * u : BANK * (u + 1)], first[s, u][:])
+        for s in range(PACK, GROUPS * PACK):
+            for u in range(S // BANK):
+                acc = bank([P, BANK])
+                for a in range(GROUPS):
+                    mother_pass(acc, s, u, a)
+                nc.scalar.copy(h[s][:, BANK * u : BANK * (u + 1)], acc[:])
+
+        f1 = [kept(f"f1_{g}", [P, PACK, NL], F32) for g in range(GROUPS)]
+        f1_codes = [kept(f"f1_codes{g}", [P, NL], U32) for g in range(GROUPS)]
+        f1_scales = [kept(f"f1_scales{g}", [P, NL], U8) for g in range(GROUPS)]
+        for g in range(GROUPS):
+            for t in range(PACK):
+                row = f1[g][:, t, :]
+                nc.vector.tensor_tensor(row, h[PACK * g + t][:].indirect(p1[:]), b[g, t][:], ALU.add)
+                nc.scalar.activation(row, row, ACT.Tanh)
+                nc.vector.tensor_scalar(row, row, gains[:, g, t : t + 1], None, ALU.mult)
+            width = HALF if g == GROUPS - 1 else NL
+            for lo in range(0, NL, width):
+                cols = slice(lo, lo + width)
+                quantise_rows(f1[g][:, :, cols], f1_codes[g][:, cols], f1_scales[g][:, cols], on_vector)
+
+        w3_codes = [kept(f"w3_codes{a}", [P, H], I32) for a in range(GROUPS)]
+        w3_plane = kept("w3_plane", [P, H], U8)
+        for a in range(GROUPS):
+            nc.vector.tensor_copy(
+                w3_codes[a][:].rearrange("p (g t c i) -> p g c t i", g=GROUPS, t=PACK, i=LINE),
+                w3_raw[a][:].rearrange("p (g c i t) -> p g c t i", g=GROUPS, t=PACK, i=LINE),
+            )
+        nc.vector.tensor_copy(
+            w3_plane[:].rearrange("p (g t m) -> p g t m", g=GROUPS, t=PACK),
+            w3_scale_raw[:].rearrange("p (g m t) -> p g t m", g=GROUPS, t=PACK),
+        )
+
+        w4q = {}
+        for a, g in w4_raw:
+            last = (a, g) == (GROUPS - 1, GROUPS - 1)
+            w4q[a, g] = quantise_weight(w4_raw[a, g], f"w4q{a}{g}", on_vector if last else on_scalar, 1 if last else 2)
+
+        per_bank = BANK // HALF
+        halves = [slice(lo, lo + HALF) for lo in range(0, NL, HALF)]
+
+        def flags(a, i):
+            return dict(start=(a == 0 and i == 0), stop=(a == GROUPS - 1 and i == per_bank - 1))
+
+        zq = {}
+        for u, cols in enumerate(halves):
+            for g in range(GROUPS):
+                rows = page([P, PACK, HALF])
                 for t0 in range(0, PACK, per_bank):
-                    acc = bank([P, per_bank, width])
-                    for a in range(2):
+                    acc = bank([P, per_bank, HALF])
+                    for a in range(GROUPS):
                         for i in range(per_bank):
                             t = t0 + i
                             w_cols = slice(GROUP * g + P * t, GROUP * g + P * (t + 1))
                             nc.tensor.matmul_mx(
                                 acc[:, i, :],
-                                lhsT=w3w[a][:, w_cols].bitcast(FP8X4),
-                                lhsT_scale=w3s[4 * a : P, w_cols],
+                                lhsT=w3_codes[a][:, w_cols].bitcast(FP8X4),
+                                lhsT_scale=w3_plane[4 * a : P, w_cols],
                                 rhs=f1_codes[a][:, cols].bitcast(FP8X4),
                                 rhs_scale=f1_scales[a][:, cols],
-                                start=(a == 0 and i == 0), stop=(a == 1 and i == per_bank - 1),
+                                **flags(a, i),
                             )
                             if a == 0:
                                 lateral_pass(acc[:, i, :], g, t, cols, False)
                     nc.scalar.activation(rows[:, t0 : t0 + per_bank, :], acc[:], ACT.Tanh)
                 for t in range(PACK):
                     nc.vector.scalar_tensor_tensor(
-                        rows[:, t, :], rows[:, t, :], gains[:, g, t : t + 1], e1[g][:, t, cols], ALU.mult, ALU.add
+                        rows[:, t, :], rows[:, t, :], gains[:, g, t : t + 1], f1[g][:, t, cols], ALU.mult, ALU.add
                     )
-                codes = kept(f"zc{lo}{g}", [P, width], U32)
-                scales = kept(f"zs{lo}{g}", [P, width], U8)
-                quantise_rows(rows[:], codes[:], scales[:], copy[g])
-                z.append((codes, scales))
-            return z
+                codes = kept(f"z_codes{u}{g}", [P, HALF], U32)
+                scales = kept(f"z_scales{u}{g}", [P, HALF], U8)
+                quantise_rows(rows[:], codes[:], scales[:], on_scalar if (u, g) == (0, 0) else on_vector)
+                zq[u, g] = codes, scales
 
-        y_scales = kept("y_scales", [P, 2, NL], U8)
-
-        def result(lo, width, z, w4q, copy, empty):
-            cols = slice(lo, lo + width)
-            per_bank = BANK // width
-            for g in range(2):
-                rows = page([P, PACK, width])
+        y_scales = kept("y_scales", [P, GROUPS, NL], U8)
+        for u, cols in enumerate(halves):
+            for g in range(GROUPS):
+                weave = on_scalar if g == 0 else on_vector
+                empty = on_vector if (u, g) == (len(halves) - 1, GROUPS - 1) else on_scalar
+                rows = page([P, PACK, HALF])
                 for t0 in range(0, PACK, per_bank):
-                    acc = bank([P, per_bank, width])
-                    for a in range(2):
+                    acc = bank([P, per_bank, HALF])
+                    for a in range(GROUPS):
                         for i in range(per_bank):
-                            t = t0 + i
-                            codes, scales = w4q[a][g]
+                            w_cols = slice(P * (t0 + i), P * (t0 + i + 1))
                             nc.tensor.matmul_mx(
                                 acc[:, i, :],
-                                lhsT=codes[:, P * t : P * (t + 1)].bitcast(FP8X4),
-                                lhsT_scale=scales[:, P * t : P * (t + 1)],
-                                rhs=z[a][0][:].bitcast(FP8X4),
-                                rhs_scale=z[a][1][:],
-                                start=(a == 0 and i == 0), stop=(a == 1 and i == per_bank - 1),
+                                lhsT=w4q[a, g][0][:, w_cols].bitcast(FP8X4),
+                                lhsT_scale=w4q[a, g][1][:, w_cols],
+                                rhs=zq[u, a][0][:].bitcast(FP8X4),
+                                rhs_scale=zq[u, a][1][:],
+                                **flags(a, i),
                             )
-                    empty[g](rows[:, t0 : t0 + per_bank, :], acc[:])
+                    empty(rows[:, t0 : t0 + per_bank, :], acc[:])
                 nc.sync.dma_start(
                     out_0[GROUP * g : GROUP * (g + 1), cols].rearrange("(p t) m -> p t m", t=PACK), rows[:]
                 )
-                y_codes = kept(f"yc{lo}{g}", [P, width], U32)
-                quantise_rows(rows[:], y_codes[:], y_scales[:, g, cols], copy[g])
-                nc.sync.dma_start(
-                    out_1[g, :, cols, :].rearrange("p m t -> p (m t)").bitcast(I32), y_codes[:].bitcast(I32)
-                )
+                y_codes = kept(f"y_codes{u}{g}", [P, HALF], U32)
+                quantise_rows(rows[:], y_codes[:], y_scales[:, g, cols], weave)
+                nc.sync.dma_start(as_words(out_1[g, :, cols, :]), y_codes[:].bitcast(I32))
 
-        w4q = [[None, None], [None, None]]
-        w4c = [[on_scalar]*2]*4
-        w4q[0][0] = quantise_weight(w4_raw[0][0], "w4q0", w4c[0])
-        w4q[1][0] = quantise_weight(w4_raw[0][1], "w4q1", w4c[1])
-        first_slope(0)
-        first_slope(1)
-        deal_w3()
-        w4q[0][1] = quantise_weight(w4_raw[1][0], "w4q2", w4c[2])
-        w4q[1][1] = quantise_weight(w4_raw[1][1], "w4q3", w4c[3])
-        chunks = [(0,256),(256,256)]
-        z = [second_slope(lo, width, [[on_scalar,on_vector],[on_vector,on_vector]][k]) for k, (lo, width) in enumerate(chunks)]
-        for k, (lo, width) in enumerate(chunks):
-            result(lo, width, z[k], w4q, [[on_scalar,on_vector],[on_scalar,on_vector]][k], [[on_scalar,on_scalar],[on_scalar,on_vector]][k])
-        for q in range(4):
+        for q in range(QUADS):
             (nc.sync, nc.scalar)[q % 2].dma_start(
                 out_2[:, 4 * q : 4 * q + 4, :].rearrange("g r m -> r g m").bitcast(I32),
                 y_scales[32 * q : 32 * q + 4, :, :].bitcast(I32),

@@ -30,6 +30,8 @@ HALF = NL // 2
 LINE = 4
 RAW_BUFS = 4
 WOVEN_BUFS = 5
+PICKED = 3
+ROW_BYTES = 4 * NL
 
 
 def tile_list_root_lateral_slopes_kernel(
@@ -42,13 +44,17 @@ def tile_list_root_lateral_slopes_kernel(
         lists = ctx.enter_context(tc.tile_pool(name="lists", bufs=1))
         keep = ctx.enter_context(tc.tile_pool(name="keep", bufs=1))
         ring = ctx.enter_context(tc.tile_pool(name="ring", bufs=1))
-        psum = ctx.enter_context(tc.psum_pool(name="psum", bufs=BANKS))
+        placed = ctx.enter_context(tc.tile_pool(name="placed", bufs=1))
+        psum = ctx.enter_context(tc.psum_pool(name="psum", bufs=1))
 
         def kept(name, shape, dtype):
             return keep.tile(shape, dtype, name=name, align_bytes=64)
 
-        def bank(shape):
-            return psum.tile(shape, F32, name="bank", tag="bank")
+        def at(name, shape, dtype, row, skip=0):
+            return placed.tile(shape, dtype, name=name, align_bytes=64, offset=row * ROW_BYTES + skip)
+
+        def bank(name, shape, number):
+            return psum.tile(shape, F32, name=name, offset=number * ROW_BYTES)
 
         def page(shape):
             return ring.tile(shape, F32, name="page", tag="page", bufs=GROUPS * PACK, align_bytes=64)
@@ -60,23 +66,25 @@ def tile_list_root_lateral_slopes_kernel(
         p1 = lists.tile([P, NL // PER_COLUMN], U16, name="p1")
         idx2 = lists.tile([P, NL // PER_COLUMN], U16, name="idx2")
 
-        w1_scale_raw = kept("w1_scale_raw", [P, GROUPS, H], U8)
-        tab_scale_rows = kept("tab_scale_rows", [P, T], U8)
+        w_scale_raw = kept("w_scale_raw", [P, GROUPS, H], U8)
+        ROWS_AT = PICKED + 7
+        tab_scale_rows = at("tab_scale_rows", [P, T], U8, ROWS_AT)
         v_scales = [kept(f"v_scales{a}", [P, S], U8) for a in range(GROUPS)]
-        tab2_scale_plane = kept("tab2_scale_plane", [P, T2], U8)
-        w3_scale_raw = kept("w3_scale_raw", [P, H], U8)
-        nc.vector.memset(tab2_scale_plane[:].bitcast(I32), 0)
+        tab2_scale_rows = kept("tab2_scale_rows", [P, T2], U8)
+        v2_scales = kept("v2_scales", [P, NL], U8)
         nc.vector.memset(tab_scale_rows[:].bitcast(I32), 0)
-        nc.gpsimd.memset(w1_scale_raw[:].rearrange("p a c -> p (a c)").bitcast(I32), 0)
+        nc.gpsimd.memset(w_scale_raw[:].rearrange("p a c -> p (a c)").bitcast(I32), 0)
+        nc.gpsimd.memset(tab2_scale_rows[:].bitcast(I32), 0)
         for a in range(GROUPS):
             nc.gpsimd.memset(v_scales[a][:].bitcast(I32), 0)
-        nc.gpsimd.memset(w3_scale_raw[:].bitcast(I32), 0)
+        nc.gpsimd.memset(v2_scales[:].bitcast(I32), 0)
 
         gains = kept("gains", [P, GROUPS, PACK], F32)
         w1_raw = kept("w1_raw", [P, GROUPS, 2 * H], U8)
         tab_sb = [kept(f"tab_sb{a}", [P, T], U32) for a in range(GROUPS)]
-        tab2_sb = kept("tab2_sb", [P, T2], U32)
-        w3_raw = [kept(f"w3_raw{a}", [P, H], I32) for a in range(GROUPS)]
+        tab2_sb = at("tab2_sb", [P, T2], U32, PICKED - 1)
+        W3_AT = PICKED + 3
+        w3_raw = at("w3_raw", [P, GROUPS, H], I32, W3_AT)
 
         def as_words(packed):
             return packed.rearrange("p n t -> p (n t)").bitcast(I32)
@@ -85,107 +93,89 @@ def tile_list_root_lateral_slopes_kernel(
             cols = slice(half * T // 2, (half + 1) * T // 2)
             nc.sync.dma_start(tab_sb[a][:, cols].bitcast(I32), as_words(tab_words[a])[:, cols])
 
-        def place_scale_rows(plane, rows):
+        def place_scale_rows(plane, rows, first):
             for q in range(QUADS):
-                nc.sync.dma_start(plane[32 * q : 32 * q + 4].bitcast(I32), rows[4 * q : 4 * q + 4].bitcast(I32))
+                lo = 32 * q + first
+                nc.sync.dma_start(plane[lo : lo + 4].bitcast(I32), rows[4 * q : 4 * q + 4].bitcast(I32))
 
         def load_weight(rows, g):
             raw = ring.tile([P, PACK, GROUP], F32, name="raw", tag="raw", bufs=RAW_BUFS)
             nc.sync.dma_start(raw[:], rows[:, g * GROUP : (g + 1) * GROUP].rearrange("(p j) c -> p j c", j=PACK))
             return raw
 
-        nc.sync.dma_start(idx2[:], offs2)
-        nc.sync.dma_start(tab2_sb[:].bitcast(I32), as_words(tab2_words[0]))
+        V2_ROW = 12
+        W3_ROW = 4
+        nc.sync.dma_start(w1_raw[:].bitcast(I32), w1_words.rearrange("a p c -> p a c").bitcast(I32))
         nc.sync.dma_start(idx[:], offs)
-        place_scale_rows(tab2_scale_plane[:], tab2_scales[0])
         nc.sync.dma_start(
             tab_scale_rows[0 : 16 * GROUPS, :].bitcast(I32), tab_scales.rearrange("a q c -> (a q) c").bitcast(I32)
         )
-        w2_raw = [load_weight(w2, 0)]
-        place_scale_rows(w1_scale_raw[:], w1_scales.rearrange("a q c -> q a c"))
-        w2_raw.append(load_weight(w2, 1))
-        nc.sync.dma_start(w1_raw[:].bitcast(I32), w1_words.rearrange("a p c -> p a c").bitcast(I32))
-        nc.sync.dma_start(p1[:], pos1)
-        nc.sync.dma_start(gains[:], gain.rearrange("(g p t) -> p g t", g=GROUPS, t=PACK))
+        place_scale_rows(w_scale_raw[:], w1_scales.rearrange("a q c -> q a c"), 0)
         load_table_half(0, 0)
+        load_table_half(0, 1)
+        place_scale_rows(w_scale_raw[:], w3_scales.rearrange("a q c -> q a c"), W3_ROW)
+        load_table_half(1, 0)
+        nc.sync.dma_start(idx2[:], offs2)
+        nc.sync.dma_start(tab2_scale_rows[0:16, :].bitcast(I32), tab2_scales[0].bitcast(I32))
         v_scale_rows = kept("v_scale_rows", [P, S], U8)
         nc.vector.tensor_copy(v_scale_rows[:], tab_scale_rows[:].indirect(idx[:]))
-        place_scale_rows(v_scales[0][:], v_scale_rows[0:16, :])
-        load_table_half(0, 1)
-        place_scale_rows(v_scales[1][:], v_scale_rows[16:32, :])
-        load_table_half(1, 0)
-        for q in range(QUADS):
-            nc.sync.dma_start(
-                w3_scale_raw[32 * q : 32 * q + 8, :].bitcast(I32), w3_scales[:, 4 * q : 4 * q + 4, :].bitcast(I32)
-            )
+        place_scale_rows(v_scales[0][:], v_scale_rows[0:16, :], 0)
         load_table_half(1, 1)
-        for a in range(GROUPS):
-            nc.sync.dma_start(w3_raw[a][:], as_words(w3_words[a]))
-        w4_raw = {(a, g): load_weight(w4[GROUP * a : GROUP * (a + 1), :], g) for g in range(GROUPS) for a in range(GROUPS)}
+        place_scale_rows(v_scales[1][:], v_scale_rows[16:32, :], 0)
+        nc.sync.dma_start(tab2_sb[:].bitcast(I32), as_words(tab2_words[0]))
+        nc.sync.dma_start(p1[:], pos1)
+        nc.sync.dma_start(gains[:], gain.rearrange("(g p t) -> p g t", g=GROUPS, t=PACK))
+        w2_raw = [load_weight(w2, 0)]
+        v2_scale_rows = kept("v2_scale_rows", [P, NL], U8)
+        nc.vector.tensor_copy(v2_scale_rows[:], tab2_scale_rows[:].indirect(idx2[:]))
+        place_scale_rows(v2_scales[:], v2_scale_rows[0:16, :], V2_ROW)
+        w2_raw.append(load_weight(w2, 1))
+        parts = [(a, g) for g in range(GROUPS) for a in range(GROUPS)]
+        w4_raw = {(a, g): load_weight(w4[GROUP * a : GROUP * (a + 1), :], g) for a, g in parts}
+        nc.sync.dma_start(w3_raw[:], w3_words.rearrange("a p n t -> p a (n t)").bitcast(I32))
 
-        w1_codes = [kept(f"w1_codes{a}", [P, 2 * H], U8) for a in range(GROUPS)]
-        w1_plane = kept("w1_plane", [P, GROUPS, H], U8)
+        v_codes = {}
+
+        def gather_mothers(a):
+            for u in range(S // BANK):
+                v_codes[a, u] = kept(f"v_codes{a}{u}", [P, BANK], U32)
+                entries = idx[:, u * BANK // PER_COLUMN : (u + 1) * BANK // PER_COLUMN]
+                nc.vector.tensor_copy(v_codes[a, u][:], tab_sb[a][:].indirect(entries))
+
+        w1_codes = [at(f"w1_codes{a}", [P, 2 * H], U8, ROWS_AT + a) for a in range(GROUPS)]
+        w_plane = [kept(f"w_plane{a}", [P, H], U8) for a in range(GROUPS)]
         for a in range(GROUPS):
             nc.vector.tensor_copy(
                 w1_codes[a][:].bitcast(U16).rearrange("p (g t m) -> p g t m", g=GROUPS, t=PACK),
                 w1_raw[:, a, :].bitcast(U16).rearrange("p (g m t) -> p g t m", g=GROUPS, t=PACK),
             )
-        nc.vector.tensor_copy(
-            w1_plane[:].rearrange("p a (g t m) -> p (a g) t m", g=GROUPS, t=PACK),
-            w1_scale_raw[:].rearrange("p a (g m t) -> p (a g) t m", g=GROUPS, t=PACK),
-        )
-
-        v_codes = {}
         for a in range(GROUPS):
-            for u in range(S // BANK):
-                v_codes[a, u] = kept(f"v_codes{a}{u}", [P, BANK], U32)
-                entries = idx[:, u * BANK // PER_COLUMN : (u + 1) * BANK // PER_COLUMN]
-                nc.vector.tensor_copy(v_codes[a, u][:], tab_sb[a][:].indirect(entries))
-        v2_codes = kept("v2_codes", [P, NL], U32)
-        v2_scales = kept("v2_scales", [P, NL], U8)
-        nc.vector.tensor_copy(v2_scales[:], tab2_scale_plane[:].indirect(idx2[:]))
-        nc.vector.tensor_copy(v2_codes[:], tab2_sb[:].indirect(idx2[:]))
+            nc.vector.tensor_copy(
+                w_plane[a][:].rearrange("p (g t m) -> p g t m", g=GROUPS, t=PACK),
+                w_scale_raw[:, a, :].rearrange("p (g m t) -> p g t m", g=GROUPS, t=PACK),
+            )
+        gather_mothers(0)
+        gather_mothers(1)
 
-        def quantise_weight(raw, name, copy, pieces):
-            staged = woven(PACK * GROUP)
-            dst = staged[:].rearrange("p (t m j) -> p m j t", t=PACK, j=PACK)
-            src = raw[:].rearrange("p j (m t) -> p m j t", t=PACK)
-            step = P // pieces
-            for m0 in range(0, P, step):
-                copy(dst[:, m0 : m0 + step], src[:, m0 : m0 + step])
-            codes = kept(name + "_codes", [P, GROUP], U32)
-            scales = kept(name + "_scales", [P, GROUP], U8)
-            nc.vector.quantize_mx(codes[:].bitcast(FP8X4), scales[:], staged[:])
-            return codes, scales
+        def round_weight(raw, staged):
+            dst = staged[:].rearrange("p (t m j) -> p m t j", t=PACK, j=PACK)
+            src = raw[:].rearrange("p j (m t) -> p m t j", t=PACK)
+            for m0 in range(0, P, P // 2):
+                nc.gpsimd.tensor_scalar(dst[:, m0 : m0 + P // 2], src[:, m0 : m0 + P // 2], 1.0, 0.0, ALU.mult, ALU.add)
+            return staged
 
-        def quantise_rows(rows, codes, scales, copy):
-            staged = woven(PACK * rows.shape[2])
+        def weave_rows(rows, copy, staged=None):
+            if staged is None:
+                staged = woven(PACK * rows.shape[2])
             copy(
                 staged[:].rearrange("p (c i t) -> p c t i", i=LINE, t=PACK),
                 rows.rearrange("p t (c i) -> p c t i", i=LINE),
             )
-            nc.vector.quantize_mx(codes.bitcast(FP8X4), scales, staged[:])
+            return staged
 
-        w2q = [quantise_weight(w2_raw[g], f"w2q{g}", on_scalar, 1) for g in range(GROUPS)]
-
-        def lateral_pass(acc, g, t, cols, alone):
-            codes, scales = w2q[g]
-            nc.tensor.matmul_mx(
-                acc,
-                lhsT=codes[:, P * t : P * (t + 1)].bitcast(FP8X4),
-                lhsT_scale=scales[:, P * t : P * (t + 1)],
-                rhs=v2_codes[:, cols].bitcast(FP8X4),
-                rhs_scale=v2_scales[:, cols],
-                start=alone, stop=alone,
-            )
-
-        b = {}
-        for g in range(GROUPS):
-            for t in range(PACK):
-                acc = bank([P, NL])
-                lateral_pass(acc[:], g, t, slice(0, NL), True)
-                b[g, t] = kept(f"b{g}{t}", [P, NL], F32)
-                nc.scalar.copy(b[g, t][:], acc[:])
+        W2_AT = ROWS_AT + 2
+        w2_staged = [round_weight(raw, at(f"w2_staged{g}", [P, PACK * GROUP], BF16, W2_AT + 2 * g)) for g, raw in enumerate(w2_raw)]
+        w4_staged = {part: round_weight(w4_raw[part], woven(PACK * GROUP)) for part in parts}
 
         h = [page([P, S]) for s in range(GROUPS * PACK)]
 
@@ -193,91 +183,147 @@ def tile_list_root_lateral_slopes_kernel(
             nc.tensor.matmul_mx(
                 acc[:],
                 lhsT=w1_codes[a][:, 2 * P * s : 2 * P * (s + 1)].bitcast(FP4X4),
-                lhsT_scale=w1_plane[:, a, P * s : P * (s + 1)],
+                lhsT_scale=w_plane[a][:, P * s : P * (s + 1)],
                 rhs=v_codes[a, u][:].bitcast(FP8X4),
                 rhs_scale=v_scales[a][:, BANK * u : BANK * (u + 1)],
                 start=(a == 0), stop=(a == GROUPS - 1),
             )
 
-        first = {(s, u): bank([P, BANK]) for u in range(S // BANK) for s in range(PACK)}
+        first = {(s, u): bank(f"h{s}{u}", [P, BANK], 2 * s + u) for u in range(S // BANK) for s in range(PACK)}
         for a in range(GROUPS):
             for (s, u), acc in first.items():
                 mother_pass(acc, s, u, a)
-        for s in range(PACK):
-            for u in range(S // BANK):
-                nc.scalar.copy(h[s][:, BANK * u : BANK * (u + 1)], first[s, u][:])
+        emptied = [(0, 0), (1, 0), (2, 0), (0, 1), (1, 1), (2, 1), (3, 0), (3, 1)]
+        for s, u in emptied:
+            (on_vector if (s, u) == (2, 0) else on_scalar)(h[s][:, BANK * u : BANK * (u + 1)], first[s, u][:])
+        free = [2 * s + u for s, u in emptied]
         for s in range(PACK, GROUPS * PACK):
             for u in range(S // BANK):
-                acc = bank([P, BANK])
+                acc = bank(f"h{s}{u}", [P, BANK], free[2 * (s - PACK) + u])
                 for a in range(GROUPS):
                     mother_pass(acc, s, u, a)
                 nc.scalar.copy(h[s][:, BANK * u : BANK * (u + 1)], acc[:])
 
+        v2_codes = kept("v2_codes", [P, NL], U32)
+        w2q = []
+
+        def quantise_w2(g):
+            codes = kept(f"w2_codes{g}", [P, GROUP], U32)
+            scales = kept(f"w2_scales{g}", [P, GROUP], U8)
+            nc.vector.quantize_mx(codes[:].bitcast(FP8X4), scales[:], w2_staged[g][:])
+            w2q.append((codes, scales))
+
+        def lateral_pass(acc, g, t, cols, start, stop):
+            codes, scales = w2q[g]
+            nc.tensor.matmul_mx(
+                acc,
+                lhsT=codes[:, P * t : P * (t + 1)].bitcast(FP8X4),
+                lhsT_scale=scales[:, P * t : P * (t + 1)],
+                rhs=v2_codes[:, cols].bitcast(FP8X4),
+                rhs_scale=v2_scales[V2_ROW:P, cols],
+                start=start, stop=stop,
+            )
+
         f1 = [kept(f"f1_{g}", [P, PACK, NL], F32) for g in range(GROUPS)]
         f1_codes = [kept(f"f1_codes{g}", [P, NL], U32) for g in range(GROUPS)]
-        f1_scales = [kept(f"f1_scales{g}", [P, NL], U8) for g in range(GROUPS)]
-        for g in range(GROUPS):
-            for t in range(PACK):
-                row = f1[g][:, t, :]
-                nc.vector.tensor_tensor(row, h[PACK * g + t][:].indirect(p1[:]), b[g, t][:], ALU.add)
-                nc.scalar.activation(row, row, ACT.Tanh)
-                nc.vector.tensor_scalar(row, row, gains[:, g, t : t + 1], None, ALU.mult)
-            width = HALF if g == GROUPS - 1 else NL
-            for lo in range(0, NL, width):
-                cols = slice(lo, lo + width)
-                quantise_rows(f1[g][:, :, cols], f1_codes[g][:, cols], f1_scales[g][:, cols], on_vector)
+        halves = [slice(lo, lo + HALF) for lo in range(0, NL, HALF)]
+        picked = {}
+        f1_staged = {}
+
+        def pick(s):
+            picked[s] = at(f"picked{s}", [P, NL], F32, {2: W2_AT, 5: W2_AT + 2}.get(s, s % 2))
+            nc.vector.tensor_copy(picked[s][:], h[s][:].indirect(p1[:]))
+
+        def first_slope(s):
+            g, t = divmod(s, PACK)
+            acc = bank(f"b{s}", [P, NL], free[s])
+            lateral_pass(acc[:], g, t, slice(0, NL), True, True)
+            row = f1[g][:, t, :]
+            nc.vector.tensor_tensor(row, acc[:], picked[s][:], ALU.add)
+            nc.scalar.activation(row, row, ACT.Tanh)
+            nc.scalar.activation(row, row, ACT.Copy, scale=gains[:, g, t : t + 1])
+
+        nc.vector.tensor_copy(v2_codes[:], tab2_sb[:].indirect(idx2[:]))
+        pick(0)
+        pick(1)
+        quantise_w2(0)
+        pick(2)
+        for s in range(GROUPS * PACK):
+            first_slope(s)
+            if s == PACK - 1:
+                quantise_w2(1)
+            if PICKED <= s + 2 < GROUPS * PACK:
+                pick(s + 2)
+            if s == PACK - 1:
+                f1_staged[0, 0] = weave_rows(f1[0][:, :, halves[0]], on_scalar)
+
+        def quantise_f1(g, u):
+            nc.vector.quantize_mx(f1_codes[g][:, halves[u]].bitcast(FP8X4), f1_scales[g][:, halves[u]], f1_staged[g, u][:])
 
         w3_codes = [kept(f"w3_codes{a}", [P, H], I32) for a in range(GROUPS)]
-        w3_plane = kept("w3_plane", [P, H], U8)
-        for a in range(GROUPS):
+
+        def deal_w3(a):
             nc.vector.tensor_copy(
                 w3_codes[a][:].rearrange("p (g t c i) -> p g c t i", g=GROUPS, t=PACK, i=LINE),
-                w3_raw[a][:].rearrange("p (g c i t) -> p g c t i", g=GROUPS, t=PACK, i=LINE),
+                w3_raw[:, a, :].rearrange("p (g c i t) -> p g c t i", g=GROUPS, t=PACK, i=LINE),
             )
-        nc.vector.tensor_copy(
-            w3_plane[:].rearrange("p (g t m) -> p g t m", g=GROUPS, t=PACK),
-            w3_scale_raw[:].rearrange("p (g m t) -> p g t m", g=GROUPS, t=PACK),
-        )
 
-        w4q = {}
-        for a, g in w4_raw:
-            last = (a, g) == (GROUPS - 1, GROUPS - 1)
-            w4q[a, g] = quantise_weight(w4_raw[a, g], f"w4q{a}{g}", on_vector if last else on_scalar, 1 if last else 2)
+        deal_w3(0)
+        deal_w3(1)
+        f1_scales = [at(f"f1_scales{g}", [P, NL], U8, W3_AT, NL * g) for g in range(GROUPS)]
+        quantise_f1(0, 0)
+        w4_scales = at("w4_scales", [P, len(parts), GROUP], U8, W3_AT + 3)
+        w4_codes = {}
+
+        def quantise_w4(n):
+            w4_codes[parts[n]] = kept(f"w4_codes{n}", [P, GROUP], U32)
+            nc.vector.quantize_mx(w4_codes[parts[n]][:].bitcast(FP8X4), w4_scales[:, n, :], w4_staged[parts[n]][:])
+
+        quantise_w4(0)
+        f1_staged[1, 0] = weave_rows(f1[1][:, :, halves[0]], on_vector, at("f1_staged", [P, PACK * HALF], BF16, W3_AT + 2))
+        f1_staged[1, 1] = weave_rows(f1[1][:, :, halves[1]], on_scalar)
+        f1_staged[0, 1] = weave_rows(f1[0][:, :, halves[1]], on_scalar, at("f1_staged2", [P, PACK * HALF], BF16, W3_AT + 1))
+        quantise_f1(1, 0)
+        quantise_w4(1)
+        quantise_f1(1, 1)
+        quantise_f1(0, 1)
 
         per_bank = BANK // HALF
-        halves = [slice(lo, lo + HALF) for lo in range(0, NL, HALF)]
-
-        def flags(a, i):
-            return dict(start=(a == 0 and i == 0), stop=(a == GROUPS - 1 and i == per_bank - 1))
 
         zq = {}
         for u, cols in enumerate(halves):
+            accs = {}
+            for g in range(GROUPS):
+                for t0 in range(0, PACK, per_bank):
+                    accs[g, t0] = bank(f"e{u}{g}{t0}", [P, per_bank, HALF], free[PACK * u + 2 * g + t0 // per_bank])
+                    for i in range(per_bank):
+                        lateral_pass(accs[g, t0][:, i, :], g, t0 + i, cols, i == 0, False)
+            for a in range(GROUPS):
+                for (g, t0), acc in accs.items():
+                    for i in range(per_bank):
+                        w_cols = slice(GROUP * g + P * (t0 + i), GROUP * g + P * (t0 + i + 1))
+                        nc.tensor.matmul_mx(
+                            acc[:, i, :],
+                            lhsT=w3_codes[a][:, w_cols].bitcast(FP8X4),
+                            lhsT_scale=w_plane[a][W3_ROW:P, w_cols],
+                            rhs=f1_codes[a][:, cols].bitcast(FP8X4),
+                            rhs_scale=f1_scales[a][:, cols],
+                            start=False, stop=(a == GROUPS - 1 and i == per_bank - 1),
+                        )
             for g in range(GROUPS):
                 rows = page([P, PACK, HALF])
                 for t0 in range(0, PACK, per_bank):
-                    acc = bank([P, per_bank, HALF])
-                    for a in range(GROUPS):
-                        for i in range(per_bank):
-                            t = t0 + i
-                            w_cols = slice(GROUP * g + P * t, GROUP * g + P * (t + 1))
-                            nc.tensor.matmul_mx(
-                                acc[:, i, :],
-                                lhsT=w3_codes[a][:, w_cols].bitcast(FP8X4),
-                                lhsT_scale=w3_plane[4 * a : P, w_cols],
-                                rhs=f1_codes[a][:, cols].bitcast(FP8X4),
-                                rhs_scale=f1_scales[a][:, cols],
-                                **flags(a, i),
-                            )
-                            if a == 0:
-                                lateral_pass(acc[:, i, :], g, t, cols, False)
-                    nc.scalar.activation(rows[:, t0 : t0 + per_bank, :], acc[:], ACT.Tanh)
+                    nc.scalar.activation(rows[:, t0 : t0 + per_bank, :], accs[g, t0][:], ACT.Tanh)
                 for t in range(PACK):
                     nc.vector.scalar_tensor_tensor(
                         rows[:, t, :], rows[:, t, :], gains[:, g, t : t + 1], f1[g][:, t, cols], ALU.mult, ALU.add
                     )
                 codes = kept(f"z_codes{u}{g}", [P, HALF], U32)
                 scales = kept(f"z_scales{u}{g}", [P, HALF], U8)
-                quantise_rows(rows[:], codes[:], scales[:], on_scalar if (u, g) == (0, 0) else on_vector)
+                staged = weave_rows(rows[:], on_scalar if (u, g) == (0, 1) else on_vector)
+                if u == 0:
+                    quantise_w4(2 + g)
+                nc.vector.quantize_mx(codes[:].bitcast(FP8X4), scales[:], staged[:])
                 zq[u, g] = codes, scales
 
         y_scales = kept("y_scales", [P, GROUPS, NL], U8)
@@ -287,24 +333,25 @@ def tile_list_root_lateral_slopes_kernel(
                 empty = on_vector if (u, g) == (len(halves) - 1, GROUPS - 1) else on_scalar
                 rows = page([P, PACK, HALF])
                 for t0 in range(0, PACK, per_bank):
-                    acc = bank([P, per_bank, HALF])
+                    acc = bank(f"y{u}{g}{t0}", [P, per_bank, HALF], free[PACK * u + 2 * g + t0 // per_bank])
                     for a in range(GROUPS):
                         for i in range(per_bank):
                             w_cols = slice(P * (t0 + i), P * (t0 + i + 1))
                             nc.tensor.matmul_mx(
                                 acc[:, i, :],
-                                lhsT=w4q[a, g][0][:, w_cols].bitcast(FP8X4),
-                                lhsT_scale=w4q[a, g][1][:, w_cols],
+                                lhsT=w4_codes[a, g][:, w_cols].bitcast(FP8X4),
+                                lhsT_scale=w4_scales[:, parts.index((a, g)), w_cols],
                                 rhs=zq[u, a][0][:].bitcast(FP8X4),
                                 rhs_scale=zq[u, a][1][:],
-                                **flags(a, i),
+                                start=(a == 0 and i == 0), stop=(a == GROUPS - 1 and i == per_bank - 1),
                             )
                     empty(rows[:, t0 : t0 + per_bank, :], acc[:])
                 nc.sync.dma_start(
                     out_0[GROUP * g : GROUP * (g + 1), cols].rearrange("(p t) m -> p t m", t=PACK), rows[:]
                 )
                 y_codes = kept(f"y_codes{u}{g}", [P, HALF], U32)
-                quantise_rows(rows[:], y_codes[:], y_scales[:, g, cols], weave)
+                staged = weave_rows(rows[:], weave)
+                nc.vector.quantize_mx(y_codes[:].bitcast(FP8X4), y_scales[:, g, cols], staged[:])
                 nc.sync.dma_start(as_words(out_1[g, :, cols, :]), y_codes[:].bitcast(I32))
 
         for q in range(QUADS):

@@ -29,7 +29,7 @@ PER_COLUMN = 16
 HALF = NL // 2
 LINE = 4
 RAW_BUFS = 4
-WOVEN_BUFS = 5
+WOVEN_BUFS = 4
 PICKED = 3
 ROW_BYTES = 4 * NL
 
@@ -67,7 +67,7 @@ def tile_list_root_lateral_slopes_kernel(
         idx2 = lists.tile([P, NL // PER_COLUMN], U16, name="idx2")
 
         w_scale_raw = kept("w_scale_raw", [P, GROUPS, H], U8)
-        ROWS_AT = PICKED + 7
+        ROWS_AT = PICKED + 9
         tab_scale_rows = at("tab_scale_rows", [P, T], U8, ROWS_AT)
         v_scales = [kept(f"v_scales{a}", [P, S], U8) for a in range(GROUPS)]
         tab2_scale_rows = kept("tab2_scale_rows", [P, T2], U8)
@@ -157,11 +157,13 @@ def tile_list_root_lateral_slopes_kernel(
         gather_mothers(0)
         gather_mothers(1)
 
-        def round_weight(raw, staged):
-            dst = staged[:].rearrange("p (t m j) -> p m t j", t=PACK, j=PACK)
-            src = raw[:].rearrange("p j (m t) -> p m t j", t=PACK)
-            for m0 in range(0, P, P // 2):
-                nc.gpsimd.tensor_scalar(dst[:, m0 : m0 + P // 2], src[:, m0 : m0 + P // 2], 1.0, 0.0, ALU.mult, ALU.add)
+        def round_weight(raw, staged, pieces, engine):
+            walk = "p m t j" if engine is nc.gpsimd else "p m j t"
+            dst = staged[:].rearrange("p (t m j) -> " + walk, t=PACK, j=PACK)
+            src = raw[:].rearrange("p j (m t) -> " + walk, t=PACK)
+            for m0 in range(0, P, P // pieces):
+                cut = slice(m0, m0 + P // pieces)
+                engine.tensor_scalar(dst[:, cut], src[:, cut], 1.0, 0.0, ALU.mult, ALU.add)
             return staged
 
         def weave_rows(rows, copy, staged=None):
@@ -174,8 +176,8 @@ def tile_list_root_lateral_slopes_kernel(
             return staged
 
         W2_AT = ROWS_AT + 2
-        w2_staged = [round_weight(raw, at(f"w2_staged{g}", [P, PACK * GROUP], BF16, W2_AT + 2 * g)) for g, raw in enumerate(w2_raw)]
-        w4_staged = {part: round_weight(w4_raw[part], woven(PACK * GROUP)) for part in parts}
+        w2_staged = [round_weight(w2_raw[0], at("w2_staged0", [P, PACK * GROUP], BF16, W2_AT), 1, nc.gpsimd)]
+        w4_staged = {}
 
         h = [page([P, S]) for s in range(GROUPS * PACK)]
 
@@ -231,7 +233,7 @@ def tile_list_root_lateral_slopes_kernel(
         f1_staged = {}
 
         def pick(s):
-            picked[s] = at(f"picked{s}", [P, NL], F32, {2: W2_AT, 5: W2_AT + 2}.get(s, s % 2))
+            picked[s] = at(f"picked{s}", [P, NL], F32, s if s < 2 else W2_AT if s == 2 else W2_AT + 1 + (s + 1) % 2)
             nc.vector.tensor_copy(picked[s][:], h[s][:].indirect(p1[:]))
 
         def first_slope(s):
@@ -247,15 +249,22 @@ def tile_list_root_lateral_slopes_kernel(
         pick(0)
         pick(1)
         quantise_w2(0)
+        w2_staged.append(round_weight(w2_raw[1], at("w2_staged1", [P, PACK * GROUP], BF16, W2_AT + 1, 64), 1, nc.gpsimd))
         pick(2)
-        for s in range(GROUPS * PACK):
+        for s in range(PACK - 1):
+            first_slope(s)
+        quantise_w2(1)
+        w4_staged[parts[0]] = round_weight(w4_raw[parts[0]], at("w4_staged", [P, PACK * GROUP], BF16, W2_AT + 3), 1, nc.gpsimd)
+        w4_staged[parts[1]] = round_weight(w4_raw[parts[1]], woven(PACK * GROUP), 1, nc.gpsimd)
+        w4_staged[parts[2]] = round_weight(w4_raw[parts[2]], woven(PACK * GROUP), 2, nc.gpsimd)
+        pick(PACK - 1)
+        pick(PACK)
+        for s in range(PACK - 1, GROUPS * PACK):
             first_slope(s)
             if s == PACK - 1:
-                quantise_w2(1)
-            if PICKED <= s + 2 < GROUPS * PACK:
-                pick(s + 2)
-            if s == PACK - 1:
                 f1_staged[0, 0] = weave_rows(f1[0][:, :, halves[0]], on_scalar)
+            if s + 2 < GROUPS * PACK:
+                pick(s + 2)
 
         def quantise_f1(g, u):
             nc.vector.quantize_mx(f1_codes[g][:, halves[u]].bitcast(FP8X4), f1_scales[g][:, halves[u]], f1_staged[g, u][:])
@@ -272,7 +281,7 @@ def tile_list_root_lateral_slopes_kernel(
         deal_w3(1)
         f1_scales = [at(f"f1_scales{g}", [P, NL], U8, W3_AT, NL * g) for g in range(GROUPS)]
         quantise_f1(0, 0)
-        w4_scales = at("w4_scales", [P, len(parts), GROUP], U8, W3_AT + 3)
+        w4_scales = at("w4_scales", [P, len(parts), GROUP], U8, W3_AT + 3, -64)
         w4_codes = {}
 
         def quantise_w4(n):
@@ -280,11 +289,12 @@ def tile_list_root_lateral_slopes_kernel(
             nc.vector.quantize_mx(w4_codes[parts[n]][:].bitcast(FP8X4), w4_scales[:, n, :], w4_staged[parts[n]][:])
 
         quantise_w4(0)
-        f1_staged[1, 0] = weave_rows(f1[1][:, :, halves[0]], on_vector, at("f1_staged", [P, PACK * HALF], BF16, W3_AT + 2))
+        f1_staged[1, 0] = weave_rows(f1[1][:, :, halves[0]], on_vector, at("f1_staged", [P, PACK * HALF], BF16, W3_AT + 2, -64))
         f1_staged[1, 1] = weave_rows(f1[1][:, :, halves[1]], on_scalar)
-        f1_staged[0, 1] = weave_rows(f1[0][:, :, halves[1]], on_scalar, at("f1_staged2", [P, PACK * HALF], BF16, W3_AT + 1))
+        f1_staged[0, 1] = weave_rows(f1[0][:, :, halves[1]], on_scalar, at("f1_staged2", [P, PACK * HALF], BF16, W3_AT + 1, -64))
         quantise_f1(1, 0)
         quantise_w4(1)
+        w4_staged[parts[3]] = round_weight(w4_raw[parts[3]], at("w4_last", [P, PACK * GROUP], BF16, W3_AT + 4, -64), 1, nc.vector)
         quantise_f1(1, 1)
         quantise_f1(0, 1)
 
@@ -346,9 +356,10 @@ def tile_list_root_lateral_slopes_kernel(
                                 start=(a == 0 and i == 0), stop=(a == GROUPS - 1 and i == per_bank - 1),
                             )
                     empty(rows[:, t0 : t0 + per_bank, :], acc[:])
-                nc.sync.dma_start(
-                    out_0[GROUP * g : GROUP * (g + 1), cols].rearrange("(p t) m -> p t m", t=PACK), rows[:]
-                )
+                    nc.sync.dma_start(
+                        out_0[GROUP * g : GROUP * (g + 1), cols].rearrange("(p t) m -> p t m", t=PACK)[:, t0 : t0 + per_bank],
+                        rows[:, t0 : t0 + per_bank, :],
+                    )
                 y_codes = kept(f"y_codes{u}{g}", [P, HALF], U32)
                 staged = weave_rows(rows[:], weave)
                 nc.vector.quantize_mx(y_codes[:].bitcast(FP8X4), y_scales[:, g, cols], staged[:])

@@ -29,7 +29,7 @@ PER_COLUMN = 16
 HALF = NL // 2
 LINE = 4
 RAW_BUFS = 4
-WOVEN_BUFS = 4
+WOVEN_BUFS = 6
 PICKED = 3
 ROW_BYTES = 4 * NL
 
@@ -83,7 +83,7 @@ def tile_list_root_lateral_slopes_kernel(
         w1_raw = kept("w1_raw", [P, GROUPS, 2 * H], U8)
         tab_sb = [kept(f"tab_sb{a}", [P, T], U32) for a in range(GROUPS)]
         tab2_sb = at("tab2_sb", [P, T2], U32, PICKED - 1)
-        W3_AT = PICKED + 3
+        W3_AT = PICKED + 4
         w3_raw = at("w3_raw", [P, GROUPS, H], I32, W3_AT)
 
         def as_words(packed):
@@ -108,27 +108,27 @@ def tile_list_root_lateral_slopes_kernel(
         nc.sync.dma_start(w1_raw[:].bitcast(I32), w1_words.rearrange("a p c -> p a c").bitcast(I32))
         nc.sync.dma_start(idx[:], offs)
         nc.sync.dma_start(
-            tab_scale_rows[0 : 16 * GROUPS, :].bitcast(I32), tab_scales.rearrange("a q c -> (a q) c").bitcast(I32)
+            tab_scale_rows[0:P:4, :].bitcast(I32), tab_scales.rearrange("a q c -> (a q) c").bitcast(I32)
         )
         place_scale_rows(w_scale_raw[:], w1_scales.rearrange("a q c -> q a c"), 0)
         load_table_half(0, 0)
-        load_table_half(0, 1)
         place_scale_rows(w_scale_raw[:], w3_scales.rearrange("a q c -> q a c"), W3_ROW)
+        load_table_half(0, 1)
         load_table_half(1, 0)
-        nc.sync.dma_start(idx2[:], offs2)
-        nc.sync.dma_start(tab2_scale_rows[0:16, :].bitcast(I32), tab2_scales[0].bitcast(I32))
         v_scale_rows = kept("v_scale_rows", [P, S], U8)
         nc.vector.tensor_copy(v_scale_rows[:], tab_scale_rows[:].indirect(idx[:]))
-        place_scale_rows(v_scales[0][:], v_scale_rows[0:16, :], 0)
+        place_scale_rows(v_scales[0][:], v_scale_rows[0 : P // 2 : 4, :], 0)
+        nc.sync.dma_start(idx2[:], offs2)
+        nc.sync.dma_start(tab2_scale_rows[P // 2 : P : 4, :].bitcast(I32), tab2_scales[0].bitcast(I32))
         load_table_half(1, 1)
-        place_scale_rows(v_scales[1][:], v_scale_rows[16:32, :], 0)
+        place_scale_rows(v_scales[1][:], v_scale_rows[P // 2 : P : 4, :], 0)
         nc.sync.dma_start(tab2_sb[:].bitcast(I32), as_words(tab2_words[0]))
         nc.sync.dma_start(p1[:], pos1)
         nc.sync.dma_start(gains[:], gain.rearrange("(g p t) -> p g t", g=GROUPS, t=PACK))
         w2_raw = [load_weight(w2, 0)]
         v2_scale_rows = kept("v2_scale_rows", [P, NL], U8)
         nc.vector.tensor_copy(v2_scale_rows[:], tab2_scale_rows[:].indirect(idx2[:]))
-        place_scale_rows(v2_scales[:], v2_scale_rows[0:16, :], V2_ROW)
+        place_scale_rows(v2_scales[:], v2_scale_rows[P // 2 : P : 4, :], V2_ROW)
         w2_raw.append(load_weight(w2, 1))
         parts = [(a, g) for g in range(GROUPS) for a in range(GROUPS)]
         w4_raw = {(a, g): load_weight(w4[GROUP * a : GROUP * (a + 1), :], g) for a, g in parts}
@@ -157,13 +157,14 @@ def tile_list_root_lateral_slopes_kernel(
         gather_mothers(0)
         gather_mothers(1)
 
-        def round_weight(raw, staged, pieces, engine):
+        def round_weight(raw, staged, engine, first=0, sets=PACK):
             walk = "p m t j" if engine is nc.gpsimd else "p m j t"
-            dst = staged[:].rearrange("p (t m j) -> " + walk, t=PACK, j=PACK)
-            src = raw[:].rearrange("p j (m t) -> " + walk, t=PACK)
-            for m0 in range(0, P, P // pieces):
-                cut = slice(m0, m0 + P // pieces)
-                engine.tensor_scalar(dst[:, cut], src[:, cut], 1.0, 0.0, ALU.mult, ALU.add)
+            dst = staged[:, first * GROUP : (first + sets) * GROUP].rearrange("p (t m j) -> " + walk, t=sets, j=PACK)
+            src = raw[:].rearrange("p j (m t) -> p j m t", t=PACK)[:, :, :, first : first + sets].rearrange("p j m t -> " + walk)
+            if engine is nc.scalar:
+                engine.copy(dst, src)
+            else:
+                engine.tensor_scalar(dst, src, 1.0, 0.0, ALU.mult, ALU.add)
             return staged
 
         def weave_rows(rows, copy, staged=None):
@@ -176,7 +177,7 @@ def tile_list_root_lateral_slopes_kernel(
             return staged
 
         W2_AT = ROWS_AT + 2
-        w2_staged = [round_weight(w2_raw[0], at("w2_staged0", [P, PACK * GROUP], BF16, W2_AT), 1, nc.gpsimd)]
+        w2_staged = [round_weight(w2_raw[0], at("w2_staged0", [P, PACK * GROUP], BF16, W2_AT), nc.gpsimd)]
         w4_staged = {}
 
         h = [page([P, S]) for s in range(GROUPS * PACK)]
@@ -226,43 +227,46 @@ def tile_list_root_lateral_slopes_kernel(
                 start=start, stop=stop,
             )
 
-        f1 = [kept(f"f1_{g}", [P, PACK, NL], F32) for g in range(GROUPS)]
+        f1 = [kept("f1_0", [P, PACK, NL], F32)]
+        E1_AT = W2_AT + 6
+        e1 = [at(f"e1_{t}", [P, NL], F32, E1_AT + t) for t in range(PACK)]
         f1_codes = [kept(f"f1_codes{g}", [P, NL], U32) for g in range(GROUPS)]
         halves = [slice(lo, lo + HALF) for lo in range(0, NL, HALF)]
         picked = {}
         f1_staged = {}
 
         def pick(s):
-            picked[s] = at(f"picked{s}", [P, NL], F32, s if s < 2 else W2_AT if s == 2 else W2_AT + 1 + (s + 1) % 2)
+            picked[s] = at(f"picked{s}", [P, NL], F32, s if s < PICKED else W2_AT if s == PICKED else W2_AT + 1 + s % 2)
             nc.vector.tensor_copy(picked[s][:], h[s][:].indirect(p1[:]))
 
         def first_slope(s):
             g, t = divmod(s, PACK)
             acc = bank(f"b{s}", [P, NL], free[s])
             lateral_pass(acc[:], g, t, slice(0, NL), True, True)
-            row = f1[g][:, t, :]
+            row = f1[0][:, t, :] if g == 0 else e1[t][:]
             nc.vector.tensor_tensor(row, acc[:], picked[s][:], ALU.add)
             nc.scalar.activation(row, row, ACT.Tanh)
-            nc.scalar.activation(row, row, ACT.Copy, scale=gains[:, g, t : t + 1])
+            if g == 0:
+                nc.scalar.activation(row, row, ACT.Copy, scale=gains[:, g, t : t + 1])
 
         nc.vector.tensor_copy(v2_codes[:], tab2_sb[:].indirect(idx2[:]))
-        pick(0)
-        pick(1)
+        for s in range(PICKED):
+            pick(s)
         quantise_w2(0)
-        w2_staged.append(round_weight(w2_raw[1], at("w2_staged1", [P, PACK * GROUP], BF16, W2_AT + 1, 64), 1, nc.gpsimd))
-        pick(2)
-        for s in range(PACK - 1):
+        w2_staged.append(round_weight(w2_raw[1], at("w2_staged1", [P, PACK * GROUP], BF16, W2_AT + 1, 64), nc.gpsimd))
+        pick(PICKED)
+        for s in range(PACK):
             first_slope(s)
+        for u in range(2):
+            f1_staged[0, u] = weave_rows(f1[0][:, :, halves[u]], on_scalar)
         quantise_w2(1)
-        w4_staged[parts[0]] = round_weight(w4_raw[parts[0]], at("w4_staged", [P, PACK * GROUP], BF16, W2_AT + 3), 1, nc.gpsimd)
-        w4_staged[parts[1]] = round_weight(w4_raw[parts[1]], woven(PACK * GROUP), 1, nc.gpsimd)
-        w4_staged[parts[2]] = round_weight(w4_raw[parts[2]], woven(PACK * GROUP), 2, nc.gpsimd)
-        pick(PACK - 1)
+        w4_staged[parts[0]] = round_weight(w4_raw[parts[0]], at("w4_staged", [P, PACK * GROUP], BF16, W2_AT + 3), nc.gpsimd)
+        w4_staged[parts[1]] = round_weight(w4_raw[parts[1]], woven(PACK * GROUP), nc.gpsimd)
+        w4_staged[parts[2]] = round_weight(w4_raw[parts[2]], woven(PACK * GROUP), nc.gpsimd, 0, 2)
         pick(PACK)
-        for s in range(PACK - 1, GROUPS * PACK):
+        pick(PACK + 1)
+        for s in range(PACK, GROUPS * PACK):
             first_slope(s)
-            if s == PACK - 1:
-                f1_staged[0, 0] = weave_rows(f1[0][:, :, halves[0]], on_scalar)
             if s + 2 < GROUPS * PACK:
                 pick(s + 2)
 
@@ -277,93 +281,136 @@ def tile_list_root_lateral_slopes_kernel(
                 w3_raw[:, a, :].rearrange("p (g c i t) -> p g c t i", g=GROUPS, t=PACK, i=LINE),
             )
 
+        round_weight(w4_raw[parts[2]], w4_staged[parts[2]], nc.scalar, 2, 2)
+        w4_staged[parts[3]] = round_weight(w4_raw[parts[3]], woven(PACK * GROUP), nc.scalar)
         deal_w3(0)
         deal_w3(1)
-        f1_scales = [at(f"f1_scales{g}", [P, NL], U8, W3_AT, NL * g) for g in range(GROUPS)]
+        f1_scales = [at("f1_scales0", [P, NL], U8, W3_AT, 64 - NL), kept("f1_scales1", [P, NL], U8)]
         quantise_f1(0, 0)
-        w4_scales = at("w4_scales", [P, len(parts), GROUP], U8, W3_AT + 3, -64)
+        f1.append(at("f1_1", [P, PACK, NL], F32, W3_AT, 64))
+        for t in range(PACK):
+            nc.vector.tensor_scalar(f1[1][:, t, :], e1[t][:], gains[:, 1, t : t + 1], None, ALU.mult)
         w4_codes = {}
+        for n, part in enumerate(parts):
+            w4_codes[part] = kept(f"w4_codes{n}", [P, GROUP], U32)
 
         def quantise_w4(n):
-            w4_codes[parts[n]] = kept(f"w4_codes{n}", [P, GROUP], U32)
             nc.vector.quantize_mx(w4_codes[parts[n]][:].bitcast(FP8X4), w4_scales[:, n, :], w4_staged[parts[n]][:])
 
-        quantise_w4(0)
-        f1_staged[1, 0] = weave_rows(f1[1][:, :, halves[0]], on_vector, at("f1_staged", [P, PACK * HALF], BF16, W3_AT + 2, -64))
+        f1_staged[1, 0] = weave_rows(f1[1][:, :, halves[0]], on_vector, at("f1_staged", [P, PACK * HALF], BF16, E1_AT, 64))
         f1_staged[1, 1] = weave_rows(f1[1][:, :, halves[1]], on_scalar)
-        f1_staged[0, 1] = weave_rows(f1[0][:, :, halves[1]], on_scalar, at("f1_staged2", [P, PACK * HALF], BF16, W3_AT + 1, -64))
         quantise_f1(1, 0)
-        quantise_w4(1)
-        w4_staged[parts[3]] = round_weight(w4_raw[parts[3]], at("w4_last", [P, PACK * GROUP], BF16, W3_AT + 4, -64), 1, nc.vector)
-        quantise_f1(1, 1)
+        w4_scales = at("w4_scales", [P, len(parts), GROUP], U8, E1_AT + 1)
+        quantise_w4(0)
         quantise_f1(0, 1)
+        quantise_w4(1)
+        quantise_w4(3)
+        quantise_f1(1, 1)
 
         per_bank = BANK // HALF
+        pairs = range(0, PACK, per_bank)
 
-        zq = {}
+        def bank_of(u, g, t0):
+            return free[PACK * u + 2 * g + t0 // per_bank]
+
+        accs = {}
         for u, cols in enumerate(halves):
-            accs = {}
             for g in range(GROUPS):
-                for t0 in range(0, PACK, per_bank):
-                    accs[g, t0] = bank(f"e{u}{g}{t0}", [P, per_bank, HALF], free[PACK * u + 2 * g + t0 // per_bank])
+                for t0 in pairs:
+                    accs[u, g, t0] = bank(f"e{u}{g}{t0}", [P, per_bank, HALF], bank_of(u, g, t0))
                     for i in range(per_bank):
-                        lateral_pass(accs[g, t0][:, i, :], g, t0 + i, cols, i == 0, False)
+                        lateral_pass(accs[u, g, t0][:, i, :], g, t0 + i, cols, i == 0, False)
             for a in range(GROUPS):
-                for (g, t0), acc in accs.items():
-                    for i in range(per_bank):
-                        w_cols = slice(GROUP * g + P * (t0 + i), GROUP * g + P * (t0 + i + 1))
+                for g in range(GROUPS):
+                    for t in range(PACK):
+                        w_cols = slice(GROUP * g + P * t, GROUP * g + P * (t + 1))
                         nc.tensor.matmul_mx(
-                            acc[:, i, :],
+                            accs[u, g, t - t % per_bank][:, t % per_bank, :],
                             lhsT=w3_codes[a][:, w_cols].bitcast(FP8X4),
                             lhsT_scale=w_plane[a][W3_ROW:P, w_cols],
                             rhs=f1_codes[a][:, cols].bitcast(FP8X4),
                             rhs_scale=f1_scales[a][:, cols],
-                            start=False, stop=(a == GROUPS - 1 and i == per_bank - 1),
+                            start=False, stop=(a == GROUPS - 1 and t % per_bank == per_bank - 1),
                         )
-            for g in range(GROUPS):
-                rows = page([P, PACK, HALF])
-                for t0 in range(0, PACK, per_bank):
-                    nc.scalar.activation(rows[:, t0 : t0 + per_bank, :], accs[g, t0][:], ACT.Tanh)
-                for t in range(PACK):
-                    nc.vector.scalar_tensor_tensor(
-                        rows[:, t, :], rows[:, t, :], gains[:, g, t : t + 1], f1[g][:, t, cols], ALU.mult, ALU.add
-                    )
-                codes = kept(f"z_codes{u}{g}", [P, HALF], U32)
-                scales = kept(f"z_scales{u}{g}", [P, HALF], U8)
-                staged = weave_rows(rows[:], on_scalar if (u, g) == (0, 1) else on_vector)
-                if u == 0:
-                    quantise_w4(2 + g)
-                nc.vector.quantize_mx(codes[:].bitcast(FP8X4), scales[:], staged[:])
-                zq[u, g] = codes, scales
 
+        z, z_staged, z_codes, z_scales = {}, {}, {}, {}
+        y, y_staged = {}, {}
         y_scales = kept("y_scales", [P, GROUPS, NL], U8)
-        for u, cols in enumerate(halves):
-            for g in range(GROUPS):
-                weave = on_scalar if g == 0 else on_vector
-                empty = on_vector if (u, g) == (len(halves) - 1, GROUPS - 1) else on_scalar
-                rows = page([P, PACK, HALF])
-                for t0 in range(0, PACK, per_bank):
-                    acc = bank(f"y{u}{g}{t0}", [P, per_bank, HALF], free[PACK * u + 2 * g + t0 // per_bank])
-                    for a in range(GROUPS):
-                        for i in range(per_bank):
-                            w_cols = slice(P * (t0 + i), P * (t0 + i + 1))
-                            nc.tensor.matmul_mx(
-                                acc[:, i, :],
-                                lhsT=w4_codes[a, g][:, w_cols].bitcast(FP8X4),
-                                lhsT_scale=w4_scales[:, parts.index((a, g)), w_cols],
-                                rhs=zq[u, a][0][:].bitcast(FP8X4),
-                                rhs_scale=zq[u, a][1][:],
-                                start=(a == 0 and i == 0), stop=(a == GROUPS - 1 and i == per_bank - 1),
-                            )
-                    empty(rows[:, t0 : t0 + per_bank, :], acc[:])
-                    nc.sync.dma_start(
-                        out_0[GROUP * g : GROUP * (g + 1), cols].rearrange("(p t) m -> p t m", t=PACK)[:, t0 : t0 + per_bank],
-                        rows[:, t0 : t0 + per_bank, :],
-                    )
-                y_codes = kept(f"y_codes{u}{g}", [P, HALF], U32)
-                staged = weave_rows(rows[:], weave)
-                nc.vector.quantize_mx(y_codes[:].bitcast(FP8X4), y_scales[:, g, cols], staged[:])
-                nc.sync.dma_start(as_words(out_1[g, :, cols, :]), y_codes[:].bitcast(I32))
+
+        def second_slope(u, g):
+            z[u, g] = page([P, PACK, HALF])
+            for t0 in pairs:
+                nc.scalar.activation(z[u, g][:, t0 : t0 + per_bank, :], accs[u, g, t0][:], ACT.Tanh)
+
+        def add_slopes(u, g):
+            for t in range(PACK):
+                row = z[u, g][:, t, :]
+                nc.vector.scalar_tensor_tensor(row, row, gains[:, g, t : t + 1], f1[g][:, t, halves[u]], ALU.mult, ALU.add)
+
+        def weave_z(u, g, copy):
+            z_staged[u, g] = weave_rows(z[u, g][:], copy)
+
+        def quantise_z(u, g):
+            z_codes[u, g] = kept(f"z_codes{u}{g}", [P, HALF], U32)
+            z_scales[u, g] = kept(f"z_scales{u}{g}", [P, HALF], U8)
+            nc.vector.quantize_mx(z_codes[u, g][:].bitcast(FP8X4), z_scales[u, g][:], z_staged[u, g][:])
+
+        def features(u, g, empty):
+            y[u, g] = page([P, PACK, HALF])
+            stored = out_0[GROUP * g : GROUP * (g + 1), halves[u]].rearrange("(p t) m -> p t m", t=PACK)
+            for t0 in pairs:
+                acc = bank(f"y{u}{g}{t0}", [P, per_bank, HALF], bank_of(u, g, t0))
+                for a in range(GROUPS):
+                    for i in range(per_bank):
+                        w_cols = slice(P * (t0 + i), P * (t0 + i + 1))
+                        nc.tensor.matmul_mx(
+                            acc[:, i, :],
+                            lhsT=w4_codes[a, g][:, w_cols].bitcast(FP8X4),
+                            lhsT_scale=w4_scales[:, parts.index((a, g)), w_cols],
+                            rhs=z_codes[u, a][:].bitcast(FP8X4),
+                            rhs_scale=z_scales[u, a][:],
+                            start=(a == 0 and i == 0), stop=(a == GROUPS - 1 and i == per_bank - 1),
+                        )
+                empty(y[u, g][:, t0 : t0 + per_bank, :], acc[:])
+                nc.sync.dma_start(stored[:, t0 : t0 + per_bank], y[u, g][:, t0 : t0 + per_bank, :])
+
+        def weave_y(u, g, copy):
+            y_staged[u, g] = weave_rows(y[u, g][:], copy)
+
+        def quantise_y(u, g):
+            y_codes = kept(f"y_codes{u}{g}", [P, HALF], U32)
+            nc.vector.quantize_mx(y_codes[:].bitcast(FP8X4), y_scales[:, g, halves[u]], y_staged[u, g][:])
+            nc.sync.dma_start(as_words(out_1[g, :, halves[u], :]), y_codes[:].bitcast(I32))
+
+        second_slope(0, 0)
+        second_slope(0, 1)
+        second_slope(1, 0)
+        add_slopes(0, 0)
+        add_slopes(0, 1)
+        weave_z(0, 0, on_scalar)
+        second_slope(1, 1)
+        weave_z(0, 1, on_vector)
+        quantise_w4(2)
+        quantise_z(0, 1)
+        quantise_z(0, 0)
+        add_slopes(1, 0)
+        features(0, 0, on_scalar)
+        add_slopes(1, 1)
+        weave_z(1, 0, on_scalar)
+        features(0, 1, on_scalar)
+        weave_z(1, 1, on_vector)
+        quantise_z(1, 0)
+        quantise_z(1, 1)
+        weave_y(0, 0, on_scalar)
+        weave_y(0, 1, on_vector)
+        features(1, 0, on_scalar)
+        quantise_y(0, 1)
+        quantise_y(0, 0)
+        features(1, 1, on_vector)
+        weave_y(1, 0, on_scalar)
+        weave_y(1, 1, on_vector)
+        quantise_y(1, 0)
+        quantise_y(1, 1)
 
         for q in range(QUADS):
             (nc.sync, nc.scalar)[q % 2].dma_start(

@@ -314,24 +314,36 @@ def tile_list_root_lateral_slopes_kernel(
             return free[PACK * u + 2 * g + t0 // per_bank]
 
         accs = {}
-        for u, cols in enumerate(halves):
+
+        def inner_pass(u, g, t, a, start):
+            w_cols = slice(GROUP * g + P * t, GROUP * g + P * (t + 1))
+            nc.tensor.matmul_mx(
+                accs[u, g, t - t % per_bank][:, t % per_bank, :],
+                lhsT=w3_codes[a][:, w_cols].bitcast(FP8X4),
+                lhsT_scale=w_plane[a][W3_ROW:P, w_cols],
+                rhs=f1_codes[a][:, halves[u]].bitcast(FP8X4),
+                rhs_scale=f1_scales[a][:, halves[u]],
+                start=start, stop=(a == GROUPS - 1 and t % per_bank == per_bank - 1),
+            )
+
+        for u in range(len(halves)):
             for g in range(GROUPS):
                 for t0 in pairs:
                     accs[u, g, t0] = bank(f"e{u}{g}{t0}", [P, per_bank, HALF], bank_of(u, g, t0))
-                    for i in range(per_bank):
-                        lateral_pass(accs[u, g, t0][:, i, :], g, t0 + i, cols, i == 0, False)
-            for a in range(GROUPS):
-                for g in range(GROUPS):
-                    for t in range(PACK):
-                        w_cols = slice(GROUP * g + P * t, GROUP * g + P * (t + 1))
-                        nc.tensor.matmul_mx(
-                            accs[u, g, t - t % per_bank][:, t % per_bank, :],
-                            lhsT=w3_codes[a][:, w_cols].bitcast(FP8X4),
-                            lhsT_scale=w_plane[a][W3_ROW:P, w_cols],
-                            rhs=f1_codes[a][:, cols].bitcast(FP8X4),
-                            rhs_scale=f1_scales[a][:, cols],
-                            start=False, stop=(a == GROUPS - 1 and t % per_bank == per_bank - 1),
-                        )
+        for g in range(GROUPS):
+            for t in range(PACK):
+                lateral_pass(accs[0, g, t - t % per_bank][:, t % per_bank, :], g, t, halves[0], t % per_bank == 0, False)
+        for a in range(GROUPS):
+            for g in range(GROUPS):
+                for t in range(PACK):
+                    inner_pass(0, g, t, a, False)
+        for g in range(GROUPS):
+            for t in range(PACK):
+                inner_pass(1, g, t, 0, t % per_bank == 0)
+            for t in range(PACK):
+                lateral_pass(accs[1, g, t - t % per_bank][:, t % per_bank, :], g, t, halves[1], False, False)
+            for t in range(PACK):
+                inner_pass(1, g, t, 1, False)
 
         z, z_staged, z_codes, z_scales = {}, {}, {}, {}
         y, y_staged = {}, {}
@@ -394,19 +406,19 @@ def tile_list_root_lateral_slopes_kernel(
         quantise_z(0, 1)
         quantise_z(0, 0)
         add_slopes(1, 0)
+        weave_z(1, 0, on_scalar)
         features(0, 0, on_scalar)
         add_slopes(1, 1)
-        weave_z(1, 0, on_scalar)
+        quantise_z(1, 0)
         features(0, 1, on_scalar)
         weave_z(1, 1, on_vector)
-        quantise_z(1, 0)
         quantise_z(1, 1)
-        weave_y(0, 0, on_scalar)
-        weave_y(0, 1, on_vector)
+        weave_y(0, 0, on_vector)
         features(1, 0, on_scalar)
-        quantise_y(0, 1)
+        weave_y(0, 1, on_vector)
         quantise_y(0, 0)
         features(1, 1, on_vector)
+        quantise_y(0, 1)
         weave_y(1, 0, on_scalar)
         weave_y(1, 1, on_vector)
         quantise_y(1, 0)

@@ -131,8 +131,9 @@ def tile_list_root_lateral_slopes_kernel(
         place_scale_rows(v2_scales[:], v2_scale_rows[P // 2 : P : 4, :], V2_ROW)
         w2_raw.append(load_weight(w2, 1))
         parts = [(a, g) for g in range(GROUPS) for a in range(GROUPS)]
-        w4_raw = {(a, g): load_weight(w4[GROUP * a : GROUP * (a + 1), :], g) for a, g in parts}
+        w4_raw = {(a, g): load_weight(w4[GROUP * a : GROUP * (a + 1), :], g) for a, g in parts[:-1]}
         nc.sync.dma_start(w3_raw[:], w3_words.rearrange("a p n t -> p a (n t)").bitcast(I32))
+        w4_raw[parts[-1]] = load_weight(w4[GROUP:, :], 1)
 
         v_codes = {}
 
@@ -157,10 +158,10 @@ def tile_list_root_lateral_slopes_kernel(
         gather_mothers(0)
         gather_mothers(1)
 
-        def round_weight(raw, staged, engine, first=0, sets=PACK):
+        def round_weight(raw, staged, engine, first=0, last=P):
             walk = "p m t j" if engine is nc.gpsimd else "p m j t"
-            dst = staged[:, first * GROUP : (first + sets) * GROUP].rearrange("p (t m j) -> " + walk, t=sets, j=PACK)
-            src = raw[:].rearrange("p j (m t) -> p j m t", t=PACK)[:, :, :, first : first + sets].rearrange("p j m t -> " + walk)
+            dst = staged[:].rearrange("p (t m j) -> " + walk, t=PACK, j=PACK)[:, first:last]
+            src = raw[:].rearrange("p j (m t) -> " + walk, t=PACK)[:, first:last]
             if engine is nc.scalar:
                 engine.copy(dst, src)
             else:
@@ -262,7 +263,7 @@ def tile_list_root_lateral_slopes_kernel(
         quantise_w2(1)
         w4_staged[parts[0]] = round_weight(w4_raw[parts[0]], at("w4_staged", [P, PACK * GROUP], BF16, W2_AT + 3), nc.gpsimd)
         w4_staged[parts[1]] = round_weight(w4_raw[parts[1]], woven(PACK * GROUP), nc.gpsimd)
-        w4_staged[parts[2]] = round_weight(w4_raw[parts[2]], woven(PACK * GROUP), nc.gpsimd, 0, 2)
+        w4_staged[parts[2]] = round_weight(w4_raw[parts[2]], woven(PACK * GROUP), nc.gpsimd, 0, 3 * P // 4)
         pick(PACK)
         pick(PACK + 1)
         for s in range(PACK, GROUPS * PACK):
@@ -281,15 +282,20 @@ def tile_list_root_lateral_slopes_kernel(
                 w3_raw[:, a, :].rearrange("p (g c i t) -> p g c t i", g=GROUPS, t=PACK, i=LINE),
             )
 
-        round_weight(w4_raw[parts[2]], w4_staged[parts[2]], nc.scalar, 2, 2)
+        round_weight(w4_raw[parts[2]], w4_staged[parts[2]], nc.scalar, 3 * P // 4)
         w4_staged[parts[3]] = round_weight(w4_raw[parts[3]], woven(PACK * GROUP), nc.scalar)
         deal_w3(0)
         deal_w3(1)
         f1_scales = [at("f1_scales0", [P, NL], U8, W3_AT, 64 - NL), kept("f1_scales1", [P, NL], U8)]
         quantise_f1(0, 0)
         f1.append(at("f1_1", [P, PACK, NL], F32, W3_AT, 64))
+
+        def gain_row(t, u):
+            nc.vector.tensor_scalar(f1[1][:, t, halves[u]], e1[t][:, halves[u]], gains[:, 1, t : t + 1], None, ALU.mult)
+
         for t in range(PACK):
-            nc.vector.tensor_scalar(f1[1][:, t, :], e1[t][:], gains[:, 1, t : t + 1], None, ALU.mult)
+            gain_row(t, 0)
+        gain_row(0, 1)
         w4_codes = {}
         for n, part in enumerate(parts):
             w4_codes[part] = kept(f"w4_codes{n}", [P, GROUP], U32)
@@ -297,10 +303,13 @@ def tile_list_root_lateral_slopes_kernel(
         def quantise_w4(n):
             nc.vector.quantize_mx(w4_codes[parts[n]][:].bitcast(FP8X4), w4_scales[:, n, :], w4_staged[parts[n]][:])
 
-        f1_staged[1, 0] = weave_rows(f1[1][:, :, halves[0]], on_vector, at("f1_staged", [P, PACK * HALF], BF16, E1_AT, 64))
-        f1_staged[1, 1] = weave_rows(f1[1][:, :, halves[1]], on_scalar)
+        f1_staged[1, 0] = weave_rows(f1[1][:, :, halves[0]], on_vector, at("f1_staged", [P, PACK * HALF], BF16, E1_AT - 1))
+        gain_row(1, 1)
         quantise_f1(1, 0)
-        w4_scales = at("w4_scales", [P, len(parts), GROUP], U8, E1_AT + 1)
+        gain_row(2, 1)
+        gain_row(3, 1)
+        f1_staged[1, 1] = weave_rows(f1[1][:, :, halves[1]], on_scalar)
+        w4_scales = at("w4_scales", [P, len(parts), GROUP], U8, E1_AT + 3)
         quantise_w4(0)
         quantise_f1(0, 1)
         quantise_w4(1)

@@ -89,8 +89,8 @@ def tile_list_root_lateral_slopes_kernel(
         def as_words(packed):
             return packed.rearrange("p n t -> p (n t)").bitcast(I32)
 
-        def load_table_half(a, half):
-            cols = slice(half * T // 2, (half + 1) * T // 2)
+        def load_table(a, lo, hi):
+            cols = slice(lo, hi)
             nc.sync.dma_start(tab_sb[a][:, cols].bitcast(I32), as_words(tab_words[a])[:, cols])
 
         def place_scale_rows(plane, rows, first):
@@ -111,20 +111,20 @@ def tile_list_root_lateral_slopes_kernel(
             tab_scale_rows[0:P:4, :].bitcast(I32), tab_scales.rearrange("a q c -> (a q) c").bitcast(I32)
         )
         place_scale_rows(w_scale_raw[:], w1_scales.rearrange("a q c -> q a c"), 0)
-        load_table_half(0, 0)
+        load_table(0, 0, T // 2)
         place_scale_rows(w_scale_raw[:], w3_scales.rearrange("a q c -> q a c"), W3_ROW)
-        load_table_half(0, 1)
-        load_table_half(1, 0)
+        nc.sync.dma_start(gains[:], gain.rearrange("(g p t) -> p g t", g=GROUPS, t=PACK))
+        nc.sync.dma_start(idx2[:], offs2)
+        load_table(0, T // 2, T)
+        load_table(1, 0, T // 4)
         v_scale_rows = kept("v_scale_rows", [P, S], U8)
         nc.vector.tensor_copy(v_scale_rows[:], tab_scale_rows[:].indirect(idx[:]))
         place_scale_rows(v_scales[0][:], v_scale_rows[0 : P // 2 : 4, :], 0)
-        nc.sync.dma_start(idx2[:], offs2)
         nc.sync.dma_start(tab2_scale_rows[P // 2 : P : 4, :].bitcast(I32), tab2_scales[0].bitcast(I32))
-        load_table_half(1, 1)
+        load_table(1, T // 4, T)
         place_scale_rows(v_scales[1][:], v_scale_rows[P // 2 : P : 4, :], 0)
         nc.sync.dma_start(tab2_sb[:].bitcast(I32), as_words(tab2_words[0]))
         nc.sync.dma_start(p1[:], pos1)
-        nc.sync.dma_start(gains[:], gain.rearrange("(g p t) -> p g t", g=GROUPS, t=PACK))
         w2_raw = [load_weight(w2, 0)]
         v2_scale_rows = kept("v2_scale_rows", [P, NL], U8)
         nc.vector.tensor_copy(v2_scale_rows[:], tab2_scale_rows[:].indirect(idx2[:]))
@@ -263,7 +263,7 @@ def tile_list_root_lateral_slopes_kernel(
         quantise_w2(1)
         w4_staged[parts[0]] = round_weight(w4_raw[parts[0]], at("w4_staged", [P, PACK * GROUP], BF16, W2_AT + 3), nc.gpsimd)
         w4_staged[parts[1]] = round_weight(w4_raw[parts[1]], woven(PACK * GROUP), nc.gpsimd)
-        w4_staged[parts[2]] = round_weight(w4_raw[parts[2]], woven(PACK * GROUP), nc.gpsimd, 0, 3 * P // 4)
+        w4_staged[parts[2]] = round_weight(w4_raw[parts[2]], woven(PACK * GROUP), nc.gpsimd, 0, 5 * P // 8)
         pick(PACK)
         pick(PACK + 1)
         for s in range(PACK, GROUPS * PACK):
@@ -282,7 +282,7 @@ def tile_list_root_lateral_slopes_kernel(
                 w3_raw[:, a, :].rearrange("p (g c i t) -> p g c t i", g=GROUPS, t=PACK, i=LINE),
             )
 
-        round_weight(w4_raw[parts[2]], w4_staged[parts[2]], nc.scalar, 3 * P // 4)
+        round_weight(w4_raw[parts[2]], w4_staged[parts[2]], nc.scalar, 5 * P // 8)
         w4_staged[parts[3]] = round_weight(w4_raw[parts[3]], woven(PACK * GROUP), nc.scalar)
         deal_w3(0)
         deal_w3(1)
@@ -319,8 +319,11 @@ def tile_list_root_lateral_slopes_kernel(
         per_bank = BANK // HALF
         pairs = range(0, PACK, per_bank)
 
+        def slope_bank(u, g, t0):
+            return free[{(0, 0): 0, (0, 1): 6, (1, 0): 2, (1, 1): 6}[u, g] + t0 // per_bank]
+
         def bank_of(u, g, t0):
-            return free[PACK * u + 2 * g + t0 // per_bank]
+            return free[{(0, 0): 0, (0, 1): 4, (1, 0): 2, (1, 1): 6}[u, g] + t0 // per_bank]
 
         accs = {}
 
@@ -338,7 +341,7 @@ def tile_list_root_lateral_slopes_kernel(
         for u in range(len(halves)):
             for g in range(GROUPS):
                 for t0 in pairs:
-                    accs[u, g, t0] = bank(f"e{u}{g}{t0}", [P, per_bank, HALF], bank_of(u, g, t0))
+                    accs[u, g, t0] = bank(f"e{u}{g}{t0}", [P, per_bank, HALF], slope_bank(u, g, t0))
         for g in range(GROUPS):
             for t in range(PACK):
                 lateral_pass(accs[0, g, t - t % per_bank][:, t % per_bank, :], g, t, halves[0], t % per_bank == 0, False)
@@ -346,7 +349,8 @@ def tile_list_root_lateral_slopes_kernel(
             for g in range(GROUPS):
                 for t in range(PACK):
                     inner_pass(0, g, t, a, False)
-        for g in range(GROUPS):
+
+        def second_half(g):
             for t in range(PACK):
                 inner_pass(1, g, t, 0, t % per_bank == 0)
             for t in range(PACK):
@@ -405,7 +409,9 @@ def tile_list_root_lateral_slopes_kernel(
 
         second_slope(0, 0)
         second_slope(0, 1)
+        second_half(0)
         second_slope(1, 0)
+        second_half(1)
         add_slopes(0, 0)
         add_slopes(0, 1)
         weave_z(0, 0, on_scalar)

@@ -94,9 +94,14 @@ def tile_list_root_lateral_slopes_kernel(
             nc.sync.dma_start(tab_sb[a][:, cols].bitcast(I32), as_words(tab_words[a])[:, cols])
 
         def place_scale_rows(plane, rows, first):
-            for q in range(QUADS):
-                lo = 32 * q + first
-                nc.sync.dma_start(plane[lo : lo + 4].bitcast(I32), rows[4 * q : 4 * q + 4].bitcast(I32))
+            for r in range(4):
+                nc.sync.dma_start(plane[first + r : P : 32].bitcast(I32), rows(r).bitcast(I32))
+
+        def stored_rows(scales):
+            return lambda r: scales.rearrange("a (q r) c -> r q a c", r=4)[r]
+
+        def spread_rows(tile, start):
+            return lambda r: tile[start + 4 * r : start + 4 * r + 49 : 16, :]
 
         def load_weight(rows, g):
             raw = ring.tile([P, PACK, GROUP], F32, name="raw", tag="raw", bufs=RAW_BUFS)
@@ -110,25 +115,25 @@ def tile_list_root_lateral_slopes_kernel(
         nc.sync.dma_start(
             tab_scale_rows[0:P:4, :].bitcast(I32), tab_scales.rearrange("a q c -> (a q) c").bitcast(I32)
         )
-        place_scale_rows(w_scale_raw[:], w1_scales.rearrange("a q c -> q a c"), 0)
+        place_scale_rows(w_scale_raw, stored_rows(w1_scales), 0)
         load_table(0, 0, T // 2)
-        place_scale_rows(w_scale_raw[:], w3_scales.rearrange("a q c -> q a c"), W3_ROW)
+        place_scale_rows(w_scale_raw, stored_rows(w3_scales), W3_ROW)
         nc.sync.dma_start(gains[:], gain.rearrange("(g p t) -> p g t", g=GROUPS, t=PACK))
         nc.sync.dma_start(idx2[:], offs2)
         load_table(0, T // 2, T)
         load_table(1, 0, T // 4)
         v_scale_rows = kept("v_scale_rows", [P, S], U8)
         nc.vector.tensor_copy(v_scale_rows[:], tab_scale_rows[:].indirect(idx[:]))
-        place_scale_rows(v_scales[0][:], v_scale_rows[0 : P // 2 : 4, :], 0)
+        place_scale_rows(v_scales[0], spread_rows(v_scale_rows, 0), 0)
         nc.sync.dma_start(tab2_scale_rows[P // 2 : P : 4, :].bitcast(I32), tab2_scales[0].bitcast(I32))
         load_table(1, T // 4, T)
-        place_scale_rows(v_scales[1][:], v_scale_rows[P // 2 : P : 4, :], 0)
+        place_scale_rows(v_scales[1], spread_rows(v_scale_rows, P // 2), 0)
         nc.sync.dma_start(tab2_sb[:].bitcast(I32), as_words(tab2_words[0]))
         nc.sync.dma_start(p1[:], pos1)
         w2_raw = [load_weight(w2, 0)]
         v2_scale_rows = kept("v2_scale_rows", [P, NL], U8)
         nc.vector.tensor_copy(v2_scale_rows[:], tab2_scale_rows[:].indirect(idx2[:]))
-        place_scale_rows(v2_scales[:], v2_scale_rows[P // 2 : P : 4, :], V2_ROW)
+        place_scale_rows(v2_scales, spread_rows(v2_scale_rows, P // 2), V2_ROW)
         w2_raw.append(load_weight(w2, 1))
         parts = [(a, g) for g in range(GROUPS) for a in range(GROUPS)]
         w4_raw = {(a, g): load_weight(w4[GROUP * a : GROUP * (a + 1), :], g) for a, g in parts[:-1]}
@@ -439,8 +444,8 @@ def tile_list_root_lateral_slopes_kernel(
         quantise_y(1, 0)
         quantise_y(1, 1)
 
-        for q in range(QUADS):
-            (nc.sync, nc.scalar)[q % 2].dma_start(
-                out_2[:, 4 * q : 4 * q + 4, :].rearrange("g r m -> r g m").bitcast(I32),
-                y_scales[32 * q : 32 * q + 4, :, :].bitcast(I32),
+        for r in range(4):
+            (nc.sync, nc.scalar)[r % 2].dma_start(
+                out_2.rearrange("g (q r) m -> r q g m", r=4)[r].bitcast(I32),
+                y_scales[r:P:32, :, :].bitcast(I32),
             )

@@ -73,7 +73,7 @@ def tile_list_root_lateral_slopes_kernel(
         tab2_scale_rows = kept("tab2_scale_rows", [P, T2], U8)
         v2_scales = kept("v2_scales", [P, NL], U8)
         nc.vector.memset(tab_scale_rows[:].bitcast(I32), 0)
-        nc.gpsimd.memset(w_scale_raw[:].rearrange("p a c -> p (a c)").bitcast(I32), 0)
+        nc.vector.memset(w_scale_raw[:].rearrange("p a c -> p (a c)").bitcast(I32), 0)
         nc.gpsimd.memset(tab2_scale_rows[:].bitcast(I32), 0)
         for a in range(GROUPS):
             nc.gpsimd.memset(v_scales[a][:].bitcast(I32), 0)
@@ -110,13 +110,13 @@ def tile_list_root_lateral_slopes_kernel(
 
         V2_ROW = 12
         W3_ROW = 4
-        nc.sync.dma_start(w1_raw[:].bitcast(I32), w1_words.rearrange("a p c -> p a c").bitcast(I32))
+        load_table(0, 0, T // 2)
         nc.sync.dma_start(idx[:], offs)
         nc.sync.dma_start(
             tab_scale_rows[0:P:4, :].bitcast(I32), tab_scales.rearrange("a q c -> (a q) c").bitcast(I32)
         )
         place_scale_rows(w_scale_raw, stored_rows(w1_scales), 0)
-        load_table(0, 0, T // 2)
+        nc.sync.dma_start(w1_raw[:].bitcast(I32), w1_words.rearrange("a p c -> p a c").bitcast(I32))
         place_scale_rows(w_scale_raw, stored_rows(w3_scales), W3_ROW)
         nc.sync.dma_start(gains[:], gain.rearrange("(g p t) -> p g t", g=GROUPS, t=PACK))
         nc.sync.dma_start(idx2[:], offs2)

@@ -80,7 +80,7 @@ def tile_list_root_lateral_slopes_kernel(
         nc.gpsimd.memset(v2_scales[:].bitcast(I32), 0)
 
         gains = kept("gains", [P, GROUPS, PACK], F32)
-        w1_raw = kept("w1_raw", [P, GROUPS, 2 * H], U8)
+        w1_raw = [kept(f"w1_raw{g}", [P, GROUPS, 2 * GROUP], U8) for g in range(GROUPS)]
         tab_sb = [kept(f"tab_sb{a}", [P, T], U32) for a in range(GROUPS)]
         tab2_sb = at("tab2_sb", [P, T2], U32, PICKED - 1)
         W3_AT = PICKED + 4
@@ -110,30 +110,35 @@ def tile_list_root_lateral_slopes_kernel(
 
         V2_ROW = 12
         W3_ROW = 4
+        def load_w1(g):
+            cols = w1_words[:, :, 2 * GROUP * g : 2 * GROUP * (g + 1)]
+            nc.sync.dma_start(w1_raw[g][:].bitcast(I32), cols.rearrange("a p c -> p a c").bitcast(I32))
+
         load_table(0, 0, T // 2)
         nc.sync.dma_start(idx[:], offs)
         nc.sync.dma_start(
             tab_scale_rows[0:P:4, :].bitcast(I32), tab_scales.rearrange("a q c -> (a q) c").bitcast(I32)
         )
         place_scale_rows(w_scale_raw, stored_rows(w1_scales), 0)
-        nc.sync.dma_start(w1_raw[:].bitcast(I32), w1_words.rearrange("a p c -> p a c").bitcast(I32))
-        place_scale_rows(w_scale_raw, stored_rows(w3_scales), W3_ROW)
-        nc.sync.dma_start(gains[:], gain.rearrange("(g p t) -> p g t", g=GROUPS, t=PACK))
-        nc.sync.dma_start(idx2[:], offs2)
         load_table(0, T // 2, T)
-        load_table(1, 0, T // 4)
+        load_w1(0)
+        place_scale_rows(w_scale_raw, stored_rows(w3_scales), W3_ROW)
+        nc.sync.dma_start(idx2[:], offs2)
+        load_table(1, 0, 3 * T // 8)
         v_scale_rows = kept("v_scale_rows", [P, S], U8)
         nc.vector.tensor_copy(v_scale_rows[:], tab_scale_rows[:].indirect(idx[:]))
         place_scale_rows(v_scales[0], spread_rows(v_scale_rows, 0), 0)
         nc.sync.dma_start(tab2_scale_rows[P // 2 : P : 4, :].bitcast(I32), tab2_scales[0].bitcast(I32))
-        load_table(1, T // 4, T)
+        load_table(1, 3 * T // 8, T)
         place_scale_rows(v_scales[1], spread_rows(v_scale_rows, P // 2), 0)
+        load_w1(1)
         nc.sync.dma_start(tab2_sb[:].bitcast(I32), as_words(tab2_words[0]))
         nc.sync.dma_start(p1[:], pos1)
         w2_raw = [load_weight(w2, 0)]
         v2_scale_rows = kept("v2_scale_rows", [P, NL], U8)
         nc.vector.tensor_copy(v2_scale_rows[:], tab2_scale_rows[:].indirect(idx2[:]))
         place_scale_rows(v2_scales, spread_rows(v2_scale_rows, P // 2), V2_ROW)
+        nc.sync.dma_start(gains[:], gain.rearrange("(g p t) -> p g t", g=GROUPS, t=PACK))
         w2_raw.append(load_weight(w2, 1))
         parts = [(a, g) for g in range(GROUPS) for a in range(GROUPS)]
         w4_raw = {(a, g): load_weight(w4[GROUP * a : GROUP * (a + 1), :], g) for a, g in parts[:-1]}
@@ -148,13 +153,16 @@ def tile_list_root_lateral_slopes_kernel(
                 entries = idx[:, u * BANK // PER_COLUMN : (u + 1) * BANK // PER_COLUMN]
                 nc.vector.tensor_copy(v_codes[a, u][:], tab_sb[a][:].indirect(entries))
 
-        w1_codes = [at(f"w1_codes{a}", [P, 2 * H], U8, ROWS_AT + a) for a in range(GROUPS)]
+        w1_codes = [at(f"w1_codes{g}", [P, GROUPS, 2 * GROUP], U8, ROWS_AT + g) for g in range(GROUPS)]
         w_plane = [kept(f"w_plane{a}", [P, H], U8) for a in range(GROUPS)]
-        for a in range(GROUPS):
-            nc.vector.tensor_copy(
-                w1_codes[a][:].bitcast(U16).rearrange("p (g t m) -> p g t m", g=GROUPS, t=PACK),
-                w1_raw[:, a, :].bitcast(U16).rearrange("p (g m t) -> p g t m", g=GROUPS, t=PACK),
+
+        def deal_w1(g, copy):
+            copy(
+                w1_codes[g][:].bitcast(U16).rearrange("p a (t m) -> p a t m", t=PACK),
+                w1_raw[g][:].bitcast(U16).rearrange("p a (m t) -> p a t m", t=PACK),
             )
+
+        deal_w1(0, on_vector)
         for a in range(GROUPS):
             nc.vector.tensor_copy(
                 w_plane[a][:].rearrange("p (g t m) -> p g t m", g=GROUPS, t=PACK),
@@ -162,6 +170,7 @@ def tile_list_root_lateral_slopes_kernel(
             )
         gather_mothers(0)
         gather_mothers(1)
+        deal_w1(1, on_vector)
 
         def round_weight(raw, staged, engine, first=0, last=P):
             walk = "p m t j" if engine is nc.gpsimd else "p m j t"
@@ -191,7 +200,7 @@ def tile_list_root_lateral_slopes_kernel(
         def mother_pass(acc, s, u, a):
             nc.tensor.matmul_mx(
                 acc[:],
-                lhsT=w1_codes[a][:, 2 * P * s : 2 * P * (s + 1)].bitcast(FP4X4),
+                lhsT=w1_codes[s // PACK][:, a, 2 * P * (s % PACK) : 2 * P * (s % PACK + 1)].bitcast(FP4X4),
                 lhsT_scale=w_plane[a][:, P * s : P * (s + 1)],
                 rhs=v_codes[a, u][:].bitcast(FP8X4),
                 rhs_scale=v_scales[a][:, BANK * u : BANK * (u + 1)],

@@ -31,6 +31,7 @@ LINE = 4
 RAW_BUFS = 4
 WOVEN_BUFS = 6
 PICKED = 3
+SHARE = P // 4
 ROW_BYTES = 4 * NL
 
 
@@ -132,9 +133,9 @@ def tile_list_root_lateral_slopes_kernel(
         load_table(1, 3 * T // 8, T)
         place_scale_rows(v_scales[1], spread_rows(v_scale_rows, P // 2), 0)
         load_w1(1)
-        nc.sync.dma_start(tab2_sb[:].bitcast(I32), as_words(tab2_words[0]))
         nc.sync.dma_start(p1[:], pos1)
         w2_raw = [load_weight(w2, 0)]
+        nc.sync.dma_start(tab2_sb[:].bitcast(I32), as_words(tab2_words[0]))
         v2_scale_rows = kept("v2_scale_rows", [P, NL], U8)
         nc.vector.tensor_copy(v2_scale_rows[:], tab2_scale_rows[:].indirect(idx2[:]))
         place_scale_rows(v2_scales, spread_rows(v2_scale_rows, P // 2), V2_ROW)
@@ -192,7 +193,7 @@ def tile_list_root_lateral_slopes_kernel(
             return staged
 
         W2_AT = ROWS_AT + 2
-        w2_staged = [round_weight(w2_raw[0], at("w2_staged0", [P, PACK * GROUP], BF16, W2_AT), nc.gpsimd)]
+        w2_staged = [round_weight(w2_raw[0], at("w2_staged0", [P, PACK * GROUP], BF16, W2_AT, 64), nc.gpsimd)]
         w4_staged = {}
 
         h = [page([P, S]) for s in range(GROUPS * PACK)]
@@ -244,40 +245,44 @@ def tile_list_root_lateral_slopes_kernel(
 
         f1 = [kept("f1_0", [P, PACK, NL], F32)]
         E1_AT = W2_AT + 6
-        e1 = [at(f"e1_{t}", [P, NL], F32, E1_AT + t) for t in range(PACK)]
+        e1 = at("e1", [P, PACK, NL], F32, E1_AT)
         f1_codes = [kept(f"f1_codes{g}", [P, NL], U32) for g in range(GROUPS)]
         halves = [slice(lo, lo + HALF) for lo in range(0, NL, HALF)]
         picked = {}
         f1_staged = {}
 
         def pick(s):
-            picked[s] = at(f"picked{s}", [P, NL], F32, s if s < PICKED else W2_AT if s == PICKED else W2_AT + 1 + s % 2)
+            row, skip = (0, 0) if s % PICKED == 0 and s < PACK else (W2_AT + s - 1, 0) if s < PACK else (W2_AT + 2 + s % 2, 64)
+            picked[s] = at(f"picked{s}", [P, NL], F32, row, skip)
             nc.vector.tensor_copy(picked[s][:], h[s][:].indirect(p1[:]))
 
         def first_slope(s):
             g, t = divmod(s, PACK)
             acc = bank(f"b{s}", [P, NL], free[s])
             lateral_pass(acc[:], g, t, slice(0, NL), True, True)
-            row = f1[0][:, t, :] if g == 0 else e1[t][:]
+            row = f1[0][:, t, :] if g == 0 else e1[:, t, :]
             nc.vector.tensor_tensor(row, acc[:], picked[s][:], ALU.add)
             nc.scalar.activation(row, row, ACT.Tanh)
-            if g == 0:
-                nc.scalar.activation(row, row, ACT.Copy, scale=gains[:, g, t : t + 1])
+            gained = row if g == 0 else row[:, halves[0]]
+            nc.scalar.activation(gained, gained, ACT.Copy, scale=gains[:, g, t : t + 1])
 
+        pick(0)
         nc.vector.tensor_copy(v2_codes[:], tab2_sb[:].indirect(idx2[:]))
-        for s in range(PICKED):
-            pick(s)
         quantise_w2(0)
-        w2_staged.append(round_weight(w2_raw[1], at("w2_staged1", [P, PACK * GROUP], BF16, W2_AT + 1, 64), nc.gpsimd))
+        w2_staged.append(round_weight(w2_raw[1], at("w2_staged1", [P, PACK * GROUP], BF16, W2_AT + 2), nc.gpsimd))
+        w4_staged[parts[0]] = round_weight(w4_raw[parts[0]], woven(PACK * GROUP), nc.gpsimd)
+        for s in range(1, PICKED):
+            pick(s)
+        first_slope(0)
         pick(PICKED)
-        for s in range(PACK):
+        for s in range(1, PACK):
             first_slope(s)
         for u in range(2):
             f1_staged[0, u] = weave_rows(f1[0][:, :, halves[u]], on_scalar)
         quantise_w2(1)
-        w4_staged[parts[0]] = round_weight(w4_raw[parts[0]], at("w4_staged", [P, PACK * GROUP], BF16, W2_AT + 3), nc.gpsimd)
-        w4_staged[parts[1]] = round_weight(w4_raw[parts[1]], woven(PACK * GROUP), nc.gpsimd)
-        w4_staged[parts[2]] = round_weight(w4_raw[parts[2]], woven(PACK * GROUP), nc.gpsimd, 0, 5 * P // 8)
+        w4_staged[parts[1]] = round_weight(w4_raw[parts[1]], at("w4_staged", [P, PACK * GROUP], BF16, W2_AT, 64), nc.gpsimd)
+        w4_staged[parts[2]] = round_weight(w4_raw[parts[2]], woven(PACK * GROUP), nc.gpsimd)
+        w4_staged[parts[3]] = round_weight(w4_raw[parts[3]], woven(PACK * GROUP), nc.gpsimd, 0, SHARE)
         pick(PACK)
         pick(PACK + 1)
         for s in range(PACK, GROUPS * PACK):
@@ -296,20 +301,17 @@ def tile_list_root_lateral_slopes_kernel(
                 w3_raw[:, a, :].rearrange("p (g c i t) -> p g c t i", g=GROUPS, t=PACK, i=LINE),
             )
 
-        round_weight(w4_raw[parts[2]], w4_staged[parts[2]], nc.scalar, 5 * P // 8)
-        w4_staged[parts[3]] = round_weight(w4_raw[parts[3]], woven(PACK * GROUP), nc.scalar)
+        round_weight(w4_raw[parts[3]], w4_staged[parts[3]], nc.scalar, SHARE)
         deal_w3(0)
         deal_w3(1)
         f1_scales = [at("f1_scales0", [P, NL], U8, W3_AT, 64 - NL), kept("f1_scales1", [P, NL], U8)]
         quantise_f1(0, 0)
-        f1.append(at("f1_1", [P, PACK, NL], F32, W3_AT, 64))
+        f1_last = at("f1_last", [P, PACK, HALF], F32, W3_AT, 64)
+        f1_rows = {(0, 0): f1[0][:, :, halves[0]], (0, 1): f1[0][:, :, halves[1]], (1, 0): e1[:, :, halves[0]], (1, 1): f1_last[:]}
 
-        def gain_row(t, u):
-            nc.vector.tensor_scalar(f1[1][:, t, halves[u]], e1[t][:, halves[u]], gains[:, 1, t : t + 1], None, ALU.mult)
+        def gain_row(t):
+            nc.vector.tensor_scalar(f1_last[:, t, :], e1[:, t, halves[1]], gains[:, 1, t : t + 1], None, ALU.mult)
 
-        for t in range(PACK):
-            gain_row(t, 0)
-        gain_row(0, 1)
         w4_codes = {}
         for n, part in enumerate(parts):
             w4_codes[part] = kept(f"w4_codes{n}", [P, GROUP], U32)
@@ -317,13 +319,13 @@ def tile_list_root_lateral_slopes_kernel(
         def quantise_w4(n):
             nc.vector.quantize_mx(w4_codes[parts[n]][:].bitcast(FP8X4), w4_scales[:, n, :], w4_staged[parts[n]][:])
 
-        f1_staged[1, 0] = weave_rows(f1[1][:, :, halves[0]], on_vector, at("f1_staged", [P, PACK * HALF], BF16, E1_AT - 1))
-        gain_row(1, 1)
+        f1_staged[1, 0] = weave_rows(f1_rows[1, 0], on_vector, at("f1_staged", [P, PACK * HALF], BF16, W3_AT + 2, 64))
+        gain_row(0)
         quantise_f1(1, 0)
-        gain_row(2, 1)
-        gain_row(3, 1)
-        f1_staged[1, 1] = weave_rows(f1[1][:, :, halves[1]], on_scalar)
-        w4_scales = at("w4_scales", [P, len(parts), GROUP], U8, E1_AT + 3)
+        for t in range(1, PACK):
+            gain_row(t)
+        f1_staged[1, 1] = weave_rows(f1_rows[1, 1], on_scalar)
+        w4_scales = at("w4_scales", [P, len(parts), GROUP], U8, W3_AT + 2, 64)
         quantise_w4(0)
         quantise_f1(0, 1)
         quantise_w4(1)
@@ -384,7 +386,7 @@ def tile_list_root_lateral_slopes_kernel(
         def add_slopes(u, g):
             for t in range(PACK):
                 row = z[u, g][:, t, :]
-                nc.vector.scalar_tensor_tensor(row, row, gains[:, g, t : t + 1], f1[g][:, t, halves[u]], ALU.mult, ALU.add)
+                nc.vector.scalar_tensor_tensor(row, row, gains[:, g, t : t + 1], f1_rows[g, u][:, t, :], ALU.mult, ALU.add)
 
         def weave_z(u, g, copy):
             z_staged[u, g] = weave_rows(z[u, g][:], copy)

from contextlib import ExitStack

import concourse.mybir as mybir

H = 1024
T, S = 4096, 1024
T2, NL = 2048, 512
FLOPS = 5368709120

F32 = mybir.dt.float32
BF16 = mybir.dt.bfloat16
I32 = mybir.dt.int32
U32 = mybir.dt.uint32
U16 = mybir.dt.uint16
U8 = mybir.dt.uint8
FP8X4 = mybir.dt.float8_e4m3fn_x4
FP4X4 = mybir.dt.float4_e2m1fn_x4
ACT = mybir.ActivationFunctionType
ALU = mybir.AluOpType

P = 128
PACK = 4
GROUP = P * PACK
GROUPS = H // GROUP
QUADS = 4
BANK = 512
BANKS = 8
PER_COLUMN = 16
HALF = NL // 2
LINE = 4
RAW_BUFS = 4
WOVEN_BUFS = 6
PICKED = 3
SHARE = P // 4
ROW_BYTES = 4 * NL


def tile_list_root_lateral_slopes_kernel(
    tc, tab_words, tab_scales, offs, pos1, tab2_words, tab2_scales, offs2,
    w1_words, w1_scales, w2, w3_words, w3_scales, gain, w4, out_0, out_1, out_2,
):
    nc = tc.nc
    on_vector, on_scalar = nc.vector.tensor_copy, nc.scalar.copy
    with ExitStack() as ctx:
        lists = ctx.enter_context(tc.tile_pool(name="lists", bufs=1))
        keep = ctx.enter_context(tc.tile_pool(name="keep", bufs=1))
        ring = ctx.enter_context(tc.tile_pool(name="ring", bufs=1))
        placed = ctx.enter_context(tc.tile_pool(name="placed", bufs=1))
        psum = ctx.enter_context(tc.psum_pool(name="psum", bufs=1))

        def kept(name, shape, dtype):
            return keep.tile(shape, dtype, name=name, align_bytes=64)

        def at(name, shape, dtype, row, skip=0):
            return placed.tile(shape, dtype, name=name, align_bytes=64, offset=row * ROW_BYTES + skip)

        def bank(name, shape, number):
            return psum.tile(shape, F32, name=name, offset=number * ROW_BYTES)

        def page(shape):
            return ring.tile(shape, F32, name="page", tag="page", bufs=GROUPS * PACK, align_bytes=64)

        def woven(width):
            return ring.tile([P, width], BF16, name="woven", tag="woven", bufs=WOVEN_BUFS, align_bytes=64)

        idx = lists.tile([P, S // PER_COLUMN], U16, name="idx")
        p1 = lists.tile([P, NL // PER_COLUMN], U16, name="p1")
        idx2 = lists.tile([P, NL // PER_COLUMN], U16, name="idx2")

        w_scale_raw = kept("w_scale_raw", [P, GROUPS, H], U8)
        ROWS_AT = PICKED + 9
        tab_scale_rows = at("tab_scale_rows", [P, T], U8, ROWS_AT)
        v_scales = [kept(f"v_scales{a}", [P, S], U8) for a in range(GROUPS)]
        tab2_scale_rows = kept("tab2_scale_rows", [P, T2], U8)
        v2_scales = kept("v2_scales", [P, NL], U8)
        nc.vector.memset(tab_scale_rows[:].bitcast(I32), 0)
        nc.vector.memset(w_scale_raw[:].rearrange("p a c -> p (a c)").bitcast(I32), 0)
        nc.gpsimd.memset(tab2_scale_rows[:].bitcast(I32), 0)
        for a in range(GROUPS):
            nc.gpsimd.memset(v_scales[a][:].bitcast(I32), 0)
        nc.gpsimd.memset(v2_scales[:].bitcast(I32), 0)

        gains = kept("gains", [P, GROUPS, PACK], F32)
        w1_raw = [kept(f"w1_raw{g}", [P, GROUPS, 2 * GROUP], U8) for g in range(GROUPS)]
        tab_sb = [kept(f"tab_sb{a}", [P, T], U32) for a in range(GROUPS)]
        tab2_sb = at("tab2_sb", [P, T2], U32, PICKED - 1)
        W3_AT = PICKED + 4
        w3_raw = at("w3_raw", [P, GROUPS, H], I32, W3_AT)

        def as_words(packed):
            return packed.rearrange("p n t -> p (n t)").bitcast(I32)

        def load_table(a, lo, hi):
            cols = slice(lo, hi)
            nc.sync.dma_start(tab_sb[a][:, cols].bitcast(I32), as_words(tab_words[a])[:, cols])

        def place_scale_rows(plane, rows, first):
            for r in range(4):
                nc.sync.dma_start(plane[first + r : P : 32].bitcast(I32), rows(r).bitcast(I32))

        def stored_rows(scales):
            return lambda r: scales.rearrange("a (q r) c -> r q a c", r=4)[r]

        def spread_rows(tile, start):
            return lambda r: tile[start + 4 * r : start + 4 * r + 49 : 16, :]

        def load_weight(rows, g):
            raw = ring.tile([P, PACK, GROUP], F32, name="raw", tag="raw", bufs=RAW_BUFS)
            nc.sync.dma_start(raw[:], rows[:, g * GROUP : (g + 1) * GROUP].rearrange("(p j) c -> p j c", j=PACK))
            return raw

        V2_ROW = 12
        W3_ROW = 4
        def load_w1(g):
            cols = w1_words[:, :, 2 * GROUP * g : 2 * GROUP * (g + 1)]
            nc.sync.dma_start(w1_raw[g][:].bitcast(I32), cols.rearrange("a p c -> p a c").bitcast(I32))

        load_table(0, 0, T // 2)
        nc.sync.dma_start(idx[:], offs)
        nc.sync.dma_start(
            tab_scale_rows[0:P:4, :].bitcast(I32), tab_scales.rearrange("a q c -> (a q) c").bitcast(I32)
        )
        place_scale_rows(w_scale_raw, stored_rows(w1_scales), 0)
        load_table(0, T // 2, T)
        load_w1(0)
        place_scale_rows(w_scale_raw, stored_rows(w3_scales), W3_ROW)
        nc.sync.dma_start(idx2[:], offs2)
        load_table(1, 0, 3 * T // 8)
        v_scale_rows = kept("v_scale_rows", [P, S], U8)
        nc.vector.tensor_copy(v_scale_rows[:], tab_scale_rows[:].indirect(idx[:]))
        place_scale_rows(v_scales[0], spread_rows(v_scale_rows, 0), 0)
        nc.sync.dma_start(tab2_scale_rows[P // 2 : P : 4, :].bitcast(I32), tab2_scales[0].bitcast(I32))
        load_table(1, 3 * T // 8, T)
        place_scale_rows(v_scales[1], spread_rows(v_scale_rows, P // 2), 0)
        load_w1(1)
        nc.sync.dma_start(p1[:], pos1)
        w2_raw = [load_weight(w2, 0)]
        nc.sync.dma_start(tab2_sb[:].bitcast(I32), as_words(tab2_words[0]))
        v2_scale_rows = kept("v2_scale_rows", [P, NL], U8)
        nc.vector.tensor_copy(v2_scale_rows[:], tab2_scale_rows[:].indirect(idx2[:]))
        place_scale_rows(v2_scales, spread_rows(v2_scale_rows, P // 2), V2_ROW)
        nc.sync.dma_start(gains[:], gain.rearrange("(g p t) -> p g t", g=GROUPS, t=PACK))
        w2_raw.append(load_weight(w2, 1))
        parts = [(a, g) for g in range(GROUPS) for a in range(GROUPS)]
        w4_raw = {(a, g): load_weight(w4[GROUP * a : GROUP * (a + 1), :], g) for a, g in parts[:-1]}
        nc.sync.dma_start(w3_raw[:], w3_words.rearrange("a p n t -> p a (n t)").bitcast(I32))
        w4_raw[parts[-1]] = load_weight(w4[GROUP:, :], 1)

        v_codes = {}

        def gather_mothers(a):
            for u in range(S // BANK):
                v_codes[a, u] = kept(f"v_codes{a}{u}", [P, BANK], U32)
                entries = idx[:, u * BANK // PER_COLUMN : (u + 1) * BANK // PER_COLUMN]
                nc.vector.tensor_copy(v_codes[a, u][:], tab_sb[a][:].indirect(entries))

        w1_codes = [at(f"w1_codes{g}", [P, GROUPS, 2 * GROUP], U8, ROWS_AT + g) for g in range(GROUPS)]
        w_plane = [kept(f"w_plane{a}", [P, H], U8) for a in range(GROUPS)]

        def deal_w1(g, copy):
            copy(
                w1_codes[g][:].bitcast(U16).rearrange("p a (t m) -> p a t m", t=PACK),
                w1_raw[g][:].bitcast(U16).rearrange("p a (m t) -> p a t m", t=PACK),
            )

        deal_w1(0, on_vector)
        for a in range(GROUPS):
            nc.vector.tensor_copy(
                w_plane[a][:].rearrange("p (g t m) -> p g t m", g=GROUPS, t=PACK),
                w_scale_raw[:, a, :].rearrange("p (g m t) -> p g t m", g=GROUPS, t=PACK),
            )
        gather_mothers(0)
        gather_mothers(1)
        deal_w1(1, on_vector)

        def round_weight(raw, staged, engine, first=0, last=P):
            walk = "p m t j" if engine is nc.gpsimd else "p m j t"
            dst = staged[:].rearrange("p (t m j) -> " + walk, t=PACK, j=PACK)[:, first:last]
            src = raw[:].rearrange("p j (m t) -> " + walk, t=PACK)[:, first:last]
            if engine is nc.scalar:
                engine.copy(dst, src)
            else:
                engine.tensor_scalar(dst, src, 1.0, 0.0, ALU.mult, ALU.add)
            return staged

        def weave_rows(rows, copy, staged=None):
            if staged is None:
                staged = woven(PACK * rows.shape[2])
            copy(
                staged[:].rearrange("p (c i t) -> p c t i", i=LINE, t=PACK),
                rows.rearrange("p t (c i) -> p c t i", i=LINE),
            )
            return staged

        W2_AT = ROWS_AT + 2
        w2_staged = [round_weight(w2_raw[0], at("w2_staged0", [P, PACK * GROUP], BF16, W2_AT, 64), nc.gpsimd)]
        w4_staged = {}

        h = [page([P, S]) for s in range(GROUPS * PACK)]

        def mother_pass(acc, s, u, a):
            nc.tensor.matmul_mx(
                acc[:],
                lhsT=w1_codes[s // PACK][:, a, 2 * P * (s % PACK) : 2 * P * (s % PACK + 1)].bitcast(FP4X4),
                lhsT_scale=w_plane[a][:, P * s : P * (s + 1)],
                rhs=v_codes[a, u][:].bitcast(FP8X4),
                rhs_scale=v_scales[a][:, BANK * u : BANK * (u + 1)],
                start=(a == 0), stop=(a == GROUPS - 1),
            )

        first = {(s, u): bank(f"h{s}{u}", [P, BANK], 2 * s + u) for u in range(S // BANK) for s in range(PACK)}
        for a in range(GROUPS):
            for (s, u), acc in first.items():
                mother_pass(acc, s, u, a)
        emptied = [(0, 0), (1, 0), (2, 0), (0, 1), (1, 1), (2, 1), (3, 0), (3, 1)]
        for s, u in emptied:
            (on_vector if (s, u) == (2, 0) else on_scalar)(h[s][:, BANK * u : BANK * (u + 1)], first[s, u][:])
        free = [2 * s + u for s, u in emptied]
        for s in range(PACK, GROUPS * PACK):
            for u in range(S // BANK):
                acc = bank(f"h{s}{u}", [P, BANK], free[2 * (s - PACK) + u])
                for a in range(GROUPS):
                    mother_pass(acc, s, u, a)
                nc.scalar.copy(h[s][:, BANK * u : BANK * (u + 1)], acc[:])

        v2_codes = kept("v2_codes", [P, NL], U32)
        w2q = []

        def quantise_w2(g):
            codes = kept(f"w2_codes{g}", [P, GROUP], U32)
            scales = kept(f"w2_scales{g}", [P, GROUP], U8)
            nc.vector.quantize_mx(codes[:].bitcast(FP8X4), scales[:], w2_staged[g][:])
            w2q.append((codes, scales))

        def lateral_pass(acc, g, t, cols, start, stop):
            codes, scales = w2q[g]
            nc.tensor.matmul_mx(
                acc,
                lhsT=codes[:, P * t : P * (t + 1)].bitcast(FP8X4),
                lhsT_scale=scales[:, P * t : P * (t + 1)],
                rhs=v2_codes[:, cols].bitcast(FP8X4),
                rhs_scale=v2_scales[V2_ROW:P, cols],
                start=start, stop=stop,
            )

        f1 = [kept("f1_0", [P, PACK, NL], F32)]
        E1_AT = W2_AT + 6
        e1 = at("e1", [P, PACK, NL], F32, E1_AT)
        f1_codes = [kept(f"f1_codes{g}", [P, NL], U32) for g in range(GROUPS)]
        halves = [slice(lo, lo + HALF) for lo in range(0, NL, HALF)]
        picked = {}
        f1_staged = {}

        def pick(s):
            row, skip = (0, 0) if s % PICKED == 0 and s < PACK else (W2_AT + s - 1, 0) if s < PACK else (W2_AT + 2 + s % 2, 64)
            picked[s] = at(f"picked{s}", [P, NL], F32, row, skip)
            nc.vector.tensor_copy(picked[s][:], h[s][:].indirect(p1[:]))

        def first_slope(s):
            g, t = divmod(s, PACK)
            acc = bank(f"b{s}", [P, NL], free[s])
            lateral_pass(acc[:], g, t, slice(0, NL), True, True)
            row = f1[0][:, t, :] if g == 0 else e1[:, t, :]
            nc.vector.tensor_tensor(row, acc[:], picked[s][:], ALU.add)
            nc.scalar.activation(row, row, ACT.Tanh)
            gained = row if g == 0 else row[:, halves[0]]
            nc.scalar.activation(gained, gained, ACT.Copy, scale=gains[:, g, t : t + 1])

        pick(0)
        nc.vector.tensor_copy(v2_codes[:], tab2_sb[:].indirect(idx2[:]))
        quantise_w2(0)
        w2_staged.append(round_weight(w2_raw[1], at("w2_staged1", [P, PACK * GROUP], BF16, W2_AT + 2), nc.gpsimd))
        w4_staged[parts[0]] = round_weight(w4_raw[parts[0]], woven(PACK * GROUP), nc.gpsimd)
        for s in range(1, PICKED):
            pick(s)
        first_slope(0)
        pick(PICKED)
        for s in range(1, PACK):
            first_slope(s)
        for u in range(2):
            f1_staged[0, u] = weave_rows(f1[0][:, :, halves[u]], on_scalar)
        quantise_w2(1)
        w4_staged[parts[1]] = round_weight(w4_raw[parts[1]], at("w4_staged", [P, PACK * GROUP], BF16, W2_AT, 64), nc.gpsimd)
        w4_staged[parts[2]] = round_weight(w4_raw[parts[2]], woven(PACK * GROUP), nc.gpsimd)
        w4_staged[parts[3]] = round_weight(w4_raw[parts[3]], woven(PACK * GROUP), nc.gpsimd, 0, SHARE)
        pick(PACK)
        pick(PACK + 1)
        for s in range(PACK, GROUPS * PACK):
            first_slope(s)
            if s + 2 < GROUPS * PACK:
                pick(s + 2)

        def quantise_f1(g, u):
            nc.vector.quantize_mx(f1_codes[g][:, halves[u]].bitcast(FP8X4), f1_scales[g][:, halves[u]], f1_staged[g, u][:])

        w3_codes = [kept(f"w3_codes{a}", [P, H], I32) for a in range(GROUPS)]

        def deal_w3(a):
            nc.vector.tensor_copy(
                w3_codes[a][:].rearrange("p (g t c i) -> p g c t i", g=GROUPS, t=PACK, i=LINE),
                w3_raw[:, a, :].rearrange("p (g c i t) -> p g c t i", g=GROUPS, t=PACK, i=LINE),
            )

        round_weight(w4_raw[parts[3]], w4_staged[parts[3]], nc.scalar, SHARE)
        deal_w3(0)
        deal_w3(1)
        f1_scales = [at("f1_scales0", [P, NL], U8, W3_AT, 64 - NL), kept("f1_scales1", [P, NL], U8)]
        quantise_f1(0, 0)
        f1_last = at("f1_last", [P, PACK, HALF], F32, W3_AT, 64)
        f1_rows = {(0, 0): f1[0][:, :, halves[0]], (0, 1): f1[0][:, :, halves[1]], (1, 0): e1[:, :, halves[0]], (1, 1): f1_last[:]}

        def gain_row(t):
            nc.vector.tensor_scalar(f1_last[:, t, :], e1[:, t, halves[1]], gains[:, 1, t : t + 1], None, ALU.mult)

        w4_codes = {}
        for n, part in enumerate(parts):
            w4_codes[part] = kept(f"w4_codes{n}", [P, GROUP], U32)

        def quantise_w4(n):
            nc.vector.quantize_mx(w4_codes[parts[n]][:].bitcast(FP8X4), w4_scales[:, n, :], w4_staged[parts[n]][:])

        f1_staged[1, 0] = weave_rows(f1_rows[1, 0], on_vector, at("f1_staged", [P, PACK * HALF], BF16, W3_AT + 2, 64))
        gain_row(0)
        quantise_f1(1, 0)
        for t in range(1, PACK):
            gain_row(t)
        f1_staged[1, 1] = weave_rows(f1_rows[1, 1], on_scalar)
        w4_scales = at("w4_scales", [P, len(parts), GROUP], U8, W3_AT + 2, 64)
        quantise_w4(0)
        quantise_f1(0, 1)
        quantise_w4(1)
        quantise_w4(3)
        quantise_f1(1, 1)

        per_bank = BANK // HALF
        pairs = range(0, PACK, per_bank)

        def slope_bank(u, g, t0):
            return free[{(0, 0): 0, (0, 1): 6, (1, 0): 2, (1, 1): 6}[u, g] + t0 // per_bank]

        def bank_of(u, g, t0):
            return free[{(0, 0): 0, (0, 1): 4, (1, 0): 2, (1, 1): 6}[u, g] + t0 // per_bank]

        accs = {}

        def inner_pass(u, g, t, a, start):
            w_cols = slice(GROUP * g + P * t, GROUP * g + P * (t + 1))
            nc.tensor.matmul_mx(
                accs[u, g, t - t % per_bank][:, t % per_bank, :],
                lhsT=w3_codes[a][:, w_cols].bitcast(FP8X4),
                lhsT_scale=w_plane[a][W3_ROW:P, w_cols],
                rhs=f1_codes[a][:, halves[u]].bitcast(FP8X4),
                rhs_scale=f1_scales[a][:, halves[u]],
                start=start, stop=(a == GROUPS - 1 and t % per_bank == per_bank - 1),
            )

        for u in range(len(halves)):
            for g in range(GROUPS):
                for t0 in pairs:
                    accs[u, g, t0] = bank(f"e{u}{g}{t0}", [P, per_bank, HALF], slope_bank(u, g, t0))
        for g in range(GROUPS):
            for t in range(PACK):
                lateral_pass(accs[0, g, t - t % per_bank][:, t % per_bank, :], g, t, halves[0], t % per_bank == 0, False)
        for a in range(GROUPS):
            for g in range(GROUPS):
                for t in range(PACK):
                    inner_pass(0, g, t, a, False)

        def second_half(g):
            for t in range(PACK):
                inner_pass(1, g, t, 0, t % per_bank == 0)
            for t in range(PACK):
                lateral_pass(accs[1, g, t - t % per_bank][:, t % per_bank, :], g, t, halves[1], False, False)
            for t in range(PACK):
                inner_pass(1, g, t, 1, False)

        z, z_staged, z_codes, z_scales = {}, {}, {}, {}
        y, y_staged = {}, {}
        y_scales = kept("y_scales", [P, GROUPS, NL], U8)

        def second_slope(u, g):
            z[u, g] = page([P, PACK, HALF])
            for t0 in pairs:
                nc.scalar.activation(z[u, g][:, t0 : t0 + per_bank, :], accs[u, g, t0][:], ACT.Tanh)

        def add_slopes(u, g):
            for t in range(PACK):
                row = z[u, g][:, t, :]
                nc.vector.scalar_tensor_tensor(row, row, gains[:, g, t : t + 1], f1_rows[g, u][:, t, :], ALU.mult, ALU.add)

        def weave_z(u, g, copy):
            z_staged[u, g] = weave_rows(z[u, g][:], copy)

        def quantise_z(u, g):
            z_codes[u, g] = kept(f"z_codes{u}{g}", [P, HALF], U32)
            z_scales[u, g] = kept(f"z_scales{u}{g}", [P, HALF], U8)
            nc.vector.quantize_mx(z_codes[u, g][:].bitcast(FP8X4), z_scales[u, g][:], z_staged[u, g][:])

        def features(u, g, empty):
            y[u, g] = page([P, PACK, HALF])
            stored = out_0[GROUP * g : GROUP * (g + 1), halves[u]].rearrange("(p t) m -> p t m", t=PACK)
            for t0 in pairs:
                acc = bank(f"y{u}{g}{t0}", [P, per_bank, HALF], bank_of(u, g, t0))
                for a in range(GROUPS):
                    for i in range(per_bank):
                        w_cols = slice(P * (t0 + i), P * (t0 + i + 1))
                        nc.tensor.matmul_mx(
                            acc[:, i, :],
                            lhsT=w4_codes[a, g][:, w_cols].bitcast(FP8X4),
                            lhsT_scale=w4_scales[:, parts.index((a, g)), w_cols],
                            rhs=z_codes[u, a][:].bitcast(FP8X4),
                            rhs_scale=z_scales[u, a][:],
                            start=(a == 0 and i == 0), stop=(a == GROUPS - 1 and i == per_bank - 1),
                        )
                empty(y[u, g][:, t0 : t0 + per_bank, :], acc[:])
                nc.sync.dma_start(stored[:, t0 : t0 + per_bank], y[u, g][:, t0 : t0 + per_bank, :])

        def weave_y(u, g, copy):
            y_staged[u, g] = weave_rows(y[u, g][:], copy)

        def quantise_y(u, g):
            y_codes = kept(f"y_codes{u}{g}", [P, HALF], U32)
            nc.vector.quantize_mx(y_codes[:].bitcast(FP8X4), y_scales[:, g, halves[u]], y_staged[u, g][:])
            nc.sync.dma_start(as_words(out_1[g, :, halves[u], :]), y_codes[:].bitcast(I32))

        second_slope(0, 0)
        second_slope(0, 1)
        second_half(0)
        second_slope(1, 0)
        second_half(1)
        add_slopes(0, 0)
        add_slopes(0, 1)
        weave_z(0, 0, on_scalar)
        second_slope(1, 1)
        weave_z(0, 1, on_vector)
        quantise_w4(2)
        quantise_z(0, 1)
        quantise_z(0, 0)
        add_slopes(1, 0)
        weave_z(1, 0, on_scalar)
        features(0, 0, on_scalar)
        add_slopes(1, 1)
        quantise_z(1, 0)
        features(0, 1, on_scalar)
        weave_z(1, 1, on_vector)
        quantise_z(1, 1)
        weave_y(0, 0, on_vector)
        features(1, 0, on_scalar)
        weave_y(0, 1, on_vector)
        quantise_y(0, 0)
        features(1, 1, on_vector)
        quantise_y(0, 1)
        weave_y(1, 0, on_scalar)
        weave_y(1, 1, on_vector)
        quantise_y(1, 0)
        quantise_y(1, 1)

        for r in range(4):
            (nc.sync, nc.scalar)[r % 2].dma_start(
                out_2.rearrange("g (q r) m -> r q g m", r=4)[r].bitcast(I32),
                y_scales[r:P:32, :, :].bitcast(I32),
            )
